import numpy as np
import ml_dtypes


def mxq(x, axis, fmt="e4m3"):
    dtype, down = {"e4m3": (ml_dtypes.float8_e4m3fn, 7), "e5m2": (ml_dtypes.float8_e5m2, 14)}[fmt]
    v = np.moveaxis(np.asarray(x, np.float32).astype(ml_dtypes.bfloat16).astype(np.float64), axis, -1)
    blocks = v.reshape(v.shape[:-1] + (-1, 32))
    amax = np.abs(blocks).max(-1, keepdims=True)
    byte = np.maximum(np.where(amax > 0, np.frexp(amax)[1] - 1 + 127, 0) - down, 1)
    scale = np.exp2(byte - 127.0)
    codes = (blocks / scale).astype(np.float32).astype(dtype).astype(np.float64)
    return np.moveaxis((codes * scale).reshape(v.shape), -1, axis)


WIDE = False


def mx_kscale(k):
    if not WIDE:
        return np.ones(k)
    levels = np.array([10, -10, 5, -5, 0])
    if k % 512:
        return np.exp2(np.random.permutation(np.resize(levels, k // 32))).repeat(32)
    a = np.empty((k // 512, 16))
    for p in range(k // 512):
        a[p, :8] = np.random.permutation(np.resize(levels, 8))
        for g in range(8):
            far = levels[np.abs(levels - a[p, g]) >= 10]
            a[p, g + 8] = far[np.random.randint(len(far))]
    return np.exp2(a.ravel()).repeat(32)


def f64(x):
    return np.asarray(x).astype(np.float64)


def striped(idx):
    return np.tile(idx.reshape(-1, 16).T, (8, 1)).astype(np.uint16)


def unstriped(offs):
    return offs[:16].T.reshape(-1).astype(np.int64)


def pack_weight(w):
    k, n = w.shape
    w = f64(np.asarray(w, np.float32).astype(ml_dtypes.bfloat16)).reshape(k // 32, 32, n)
    amax = np.abs(w).max(1)
    byte = np.clip(np.where(amax > 0, np.frexp(amax)[1] - 1 + 127 - 7, 1), 1, 254)
    scaled = (w * np.exp2(127.0 - byte)[:, None, :]).reshape(k, n).astype(np.float32)
    words = np.ascontiguousarray(scaled.reshape(k // 512, 128, 4, n).transpose(0, 1, 3, 2)).astype(ml_dtypes.float8_e4m3fn).view(np.uint8)
    return words, np.ascontiguousarray(byte.astype(np.uint8).reshape(k // 512, 16, n))


def unpack_weight(words, scales):
    g, p, n, _ = words.shape
    vals = np.ascontiguousarray(words).view(ml_dtypes.float8_e4m3fn).astype(np.float64) * np.repeat(np.exp2(scales.astype(np.float64) - 127.0), 8, axis=1)[..., None]
    return vals.transpose(0, 1, 3, 2).reshape(g * 512, n)


def sigmoid(v):
    return 1.0 / (1.0 + np.exp(-np.maximum(v, -700.0)))


K, T, S, N = 512, 2048, 1024, 128


def setup_inputs():
    n = np.random.standard_normal
    s = mx_kscale(K)[:, None]
    packed_w1 = pack_weight(n((K, N)) / np.sqrt(K) / s)
    packed_w2 = pack_weight(n((K, N)) / np.sqrt(K) / s)
    packed_w3 = pack_weight(n((K, N)) / np.sqrt(K) / s)
    return {
        "xT": (n((K, T)) * s).astype(np.float32),
        "w1_words": packed_w1[0],
        "w1_scales": packed_w1[1],
        "w2_words": packed_w2[0],
        "w2_scales": packed_w2[1],
        "w3_words": packed_w3[0],
        "w3_scales": packed_w3[1],
        "cell": n((N, T)).astype(np.float32),
        "offs": striped(np.random.permutation(T)[(T * np.random.uniform(0, 1, S) ** 4).astype(np.int64)]),
    }


def reference(xT, w1_words, w1_scales, w2_words, w2_scales, w3_words, w3_scales, cell, offs):
    xq = mxq(f64(xT)[:, unstriped(offs)], 0, "e4m3")
    f = sigmoid(unpack_weight(w1_words, w1_scales).T @ xq)
    r = f64(cell)[:, unstriped(offs)]
    i = sigmoid(unpack_weight(w2_words, w2_scales).T @ xq)
    g = np.tanh(unpack_weight(w3_words, w3_scales).T @ xq)
    return f * r + i * g

@@ -1,0 +1,124 @@
+from contextlib import ExitStack
+
+import concourse.mybir as mybir
+
+K, T, S, N = 512, 2048, 1024, 128
+FLOPS = 3 * 2 * K * N * S
+
+F32 = mybir.dt.float32
+BF16 = mybir.dt.bfloat16
+I32 = mybir.dt.int32
+U32 = mybir.dt.uint32
+U16 = mybir.dt.uint16
+U8 = mybir.dt.uint8
+FP8X4 = mybir.dt.float8_e4m3fn_x4
+ACT = mybir.ActivationFunctionType
+ALU = mybir.AluOpType
+
+P = 128
+LOAD = 512
+CHUNK = 256
+LAST_VECTOR = 352
+
+
+def tile_picked_beamcell_none_l_kernel(
+    tc, xT, w1_words, w1_scales, w2_words, w2_scales, w3_words, w3_scales, cell, offs, out
+):
+    nc = tc.nc
+    with ExitStack() as ctx:
+        keep = ctx.enter_context(tc.tile_pool(name="keep", bufs=1))
+        psum = ctx.enter_context(tc.psum_pool(name="psum", bufs=1))
+
+        offsets = keep.tile([P, S // 16], U16, name="offsets")
+        x_rows = xT.rearrange("(p h e) c -> p h e c", h=2, e=2)
+        loads = T // LOAD
+        raw = {}
+        for h in range(2):
+            for c in range(loads):
+                raw[h, c] = keep.tile([P, 2, LOAD], F32, name="raw_%d_%d" % (h, c))
+                nc.sync.dma_start(out=raw[h, c][:], in_=x_rows[:, h, :, c * LOAD:(c + 1) * LOAD])
+                if (h, c) == (0, 1):
+                    nc.sync.dma_start(offsets[:], offs)
+        w_codes = keep.tile([P, 3, N], U32, name="w_codes", align_bytes=64)
+        for g, words in enumerate((w1_words, w2_words, w3_words)):
+            nc.sync.dma_start(
+                out=w_codes[:, g, :].bitcast(I32), in_=words[0].rearrange("p n t -> p (n t)").bitcast(I32)
+            )
+        cell_sb = keep.tile([P, T], F32, name="cell_sb")
+        nc.sync.dma_start(out=cell_sb[:], in_=cell)
+
+        w_planes = keep.tile([P, 3 * N], U8, name="w_planes", align_bytes=64)
+        nc.gpsimd.memset(w_planes[:].bitcast(I32), 0)
+        for g, scales in enumerate((w1_scales, w2_scales, w3_scales)):
+            nc.gpsimd.dma_start(out=w_planes[0:16, g * N:(g + 1) * N].bitcast(I32), in_=scales[0].bitcast(I32))
+        for q in range(1, 4):
+            nc.gpsimd.dma_start(
+                out=w_planes[32 * q:32 * q + 4, :].bitcast(I32), in_=w_planes[4 * q:4 * q + 4, :].bitcast(I32)
+            )
+
+        pairs = [keep.tile([P, T], U32, name="pairs_%d" % h) for h in range(2)]
+
+        def cast(engine_copy, h, c, a, b):
+            dst = pairs[h][:, c * LOAD + a:c * LOAD + b].bitcast(BF16).rearrange("p (c e) -> p c e", e=2)
+            engine_copy(out=dst, in_=raw[h, c][:, :, a:b].rearrange("p e c -> p c e"))
+
+        picked = keep.tile([P, 2, S], U32, name="picked")
+        for c in range(loads):
+            cast(nc.vector.tensor_copy, 0, c, 0, LOAD)
+        nc.vector.tensor_copy(picked[:, 0, :], pairs[0][:].indirect(offsets[:]))
+        cast(nc.scalar.copy, 1, 0, 0, LOAD)
+        cast(nc.scalar.copy, 1, 1, 0, LOAD)
+        cast(nc.vector.tensor_copy, 1, 2, 0, LOAD)
+        cast(nc.vector.tensor_copy, 1, 3, 0, LAST_VECTOR)
+        cast(nc.scalar.copy, 1, 3, LAST_VECTOR, LOAD)
+
+        chunks = S // CHUNK
+
+        def entries(j):
+            return offsets[:, j * CHUNK // 16:(j + 1) * CHUNK // 16]
+
+        woven = []
+        for j in range(chunks):
+            cols = slice(j * CHUNK, (j + 1) * CHUNK)
+            nc.vector.tensor_copy(picked[:, 1, cols], pairs[1][:].indirect(entries(j)))
+            tile = keep.tile([P, CHUNK, 2], U32, name="woven_%d" % j, align_bytes=64)
+            nc.scalar.copy(out=tile[:], in_=picked[:, :, cols].rearrange("p h n -> p n h"))
+            woven.append(tile)
+
+        gates, fresh = [], []
+        for j in range(chunks):
+            codes = keep.tile([P, CHUNK], U32, name="codes_%d" % j, align_bytes=64)
+            plane = keep.tile([P, CHUNK], U8, name="plane_%d" % j, align_bytes=64)
+            nc.vector.quantize_mx(
+                out=codes[:].bitcast(FP8X4),
+                scales=plane[:],
+                in_=woven[j][:].rearrange("p n h -> p (n h)").bitcast(BF16),
+            )
+            bank_fq = psum.tile([P, 2 * CHUNK], F32, name="bank_fq_%d" % j)
+            bank_g = psum.tile([P, CHUNK], F32, name="bank_g_%d" % j)
+            for g, dst in enumerate((bank_fq[:, 0:CHUNK], bank_fq[:, CHUNK:2 * CHUNK], bank_g[:])):
+                nc.tensor.matmul_mx(
+                    out=dst,
+                    lhsT=w_codes[:, g, :].bitcast(FP8X4),
+                    lhsT_scale=w_planes[:, g * N:(g + 1) * N],
+                    rhs=codes[:].bitcast(FP8X4),
+                    rhs_scale=plane[:],
+                    start=True,
+                    stop=True,
+                )
+            fq = keep.tile([P, 2 * CHUNK], F32, name="fq_%d" % j)
+            cg = keep.tile([P, 2 * CHUNK], F32, name="cg_%d" % j)
+            nc.scalar.activation(fq[:], bank_fq[:], ACT.Sigmoid)
+            nc.scalar.activation(cg[:, CHUNK:2 * CHUNK], bank_g[:], ACT.Tanh)
+            gates.append(fq)
+            fresh.append(cg)
+
+        for j in range(chunks):
+            nc.vector.tensor_copy(fresh[j][:, 0:CHUNK], cell_sb[:].indirect(entries(j)))
+        for j in range(chunks):
+            cols = slice(j * CHUNK, (j + 1) * CHUNK)
+            terms = keep.tile([P, 2 * CHUNK], F32, name="terms_%d" % j)
+            nc.vector.tensor_tensor(terms[:], gates[j][:], fresh[j][:], ALU.mult)
+            result = keep.tile([P, CHUNK], F32, name="result_%d" % j)
+            nc.vector.tensor_tensor(result[:], terms[:, 0:CHUNK], terms[:, CHUNK:2 * CHUNK], ALU.add)
+            nc.sync.dma_start(out=out[:, cols], in_=result[:])

@@ -16,9 +16,7 @@ ACT = mybir.ActivationFunctionType
 ALU = mybir.AluOpType
 
 P = 128
-LOAD = 512
 CHUNK = 256
-LAST_VECTOR = 352
 
 
 def tile_picked_beamcell_none_l_kernel(
@@ -29,96 +27,144 @@ def tile_picked_beamcell_none_l_kernel(
         keep = ctx.enter_context(tc.tile_pool(name="keep", bufs=1))
         psum = ctx.enter_context(tc.psum_pool(name="psum", bufs=1))
 
+        w_planes = keep.tile([P, 3 * N], U8, name="w_planes", align_bytes=64)
+        nc.vector.memset(w_planes[:].bitcast(I32), 0)
+
+        warm = keep.tile([P, 2], F32, name="warm")
+        nc.vector.memset(warm[:, 0:1], 0.0)
+        nc.scalar.activation(warm[:, 1:2], warm[:, 0:1], ACT.Sigmoid)
+
         offsets = keep.tile([P, S // 16], U16, name="offsets")
-        x_rows = xT.rearrange("(p h e) c -> p h e c", h=2, e=2)
-        loads = T // LOAD
-        raw = {}
-        for h in range(2):
-            for c in range(loads):
-                raw[h, c] = keep.tile([P, 2, LOAD], F32, name="raw_%d_%d" % (h, c))
-                nc.sync.dma_start(out=raw[h, c][:], in_=x_rows[:, h, :, c * LOAD:(c + 1) * LOAD])
-                if (h, c) == (0, 1):
-                    nc.sync.dma_start(offsets[:], offs)
+        x_rows = xT.rearrange("(p t) c -> p t c", t=4)
+
+        raw_2 = []
+        for half in range(2):
+            tile = keep.tile([P, T // 2], F32, name="raw_2_%d" % half)
+            nc.sync.dma_start(out=tile[:], in_=x_rows[:, 2, half * T // 2:(half + 1) * T // 2])
+            raw_2.append(tile)
+        nc.sync.dma_start(offsets[:], offs)
+        raw_01 = []
+        for half in range(2):
+            tile = keep.tile([P, 2, T // 2], F32, name="raw_01_%d" % half)
+            nc.sync.dma_start(out=tile[:], in_=x_rows[:, 0:2, half * T // 2:(half + 1) * T // 2])
+            raw_01.append(tile)
+            if half == 0:
+                for g, scales in enumerate((w1_scales, w2_scales, w3_scales)):
+                    nc.sync.dma_start(
+                        out=w_planes[0:16, g * N:(g + 1) * N].bitcast(I32), in_=scales[0].bitcast(I32)
+                    )
+        raw_3 = []
+        for piece in range(4):
+            tile = keep.tile([P, T // 4], F32, name="raw_3_%d" % piece)
+            nc.sync.dma_start(out=tile[:], in_=x_rows[:, 3, piece * T // 4:(piece + 1) * T // 4])
+            raw_3.append(tile)
+        for q in range(1, 4):
+            nc.sync.dma_start(
+                out=w_planes[32 * q:32 * q + 4, :].bitcast(I32), in_=w_planes[4 * q:4 * q + 4, :].bitcast(I32)
+            )
+        cell_sb = keep.tile([P, T], F32, name="cell_sb")
+        nc.sync.dma_start(out=cell_sb[:], in_=cell)
         w_codes = keep.tile([P, 3, N], U32, name="w_codes", align_bytes=64)
         for g, words in enumerate((w1_words, w2_words, w3_words)):
             nc.sync.dma_start(
                 out=w_codes[:, g, :].bitcast(I32), in_=words[0].rearrange("p n t -> p (n t)").bitcast(I32)
             )
-        cell_sb = keep.tile([P, T], F32, name="cell_sb")
-        nc.sync.dma_start(out=cell_sb[:], in_=cell)
 
-        w_planes = keep.tile([P, 3 * N], U8, name="w_planes", align_bytes=64)
-        nc.gpsimd.memset(w_planes[:].bitcast(I32), 0)
-        for g, scales in enumerate((w1_scales, w2_scales, w3_scales)):
-            nc.gpsimd.dma_start(out=w_planes[0:16, g * N:(g + 1) * N].bitcast(I32), in_=scales[0].bitcast(I32))
-        for q in range(1, 4):
-            nc.gpsimd.dma_start(
-                out=w_planes[32 * q:32 * q + 4, :].bitcast(I32), in_=w_planes[4 * q:4 * q + 4, :].bitcast(I32)
-            )
+        def entries(a, b):
+            return offsets[:, a // 16:b // 16]
 
-        pairs = [keep.tile([P, T], U32, name="pairs_%d" % h) for h in range(2)]
+        runs = [(0, 256), (256, 512), (512, 1024)]
+        woven = [
+            keep.tile([P, b - a, 4], BF16, name="woven_%d" % r, tag="woven_%d" % r, align_bytes=64)
+            for r, (a, b) in enumerate(runs)
+        ]
 
-        def cast(engine_copy, h, c, a, b):
-            dst = pairs[h][:, c * LOAD + a:c * LOAD + b].bitcast(BF16).rearrange("p (c e) -> p c e", e=2)
-            engine_copy(out=dst, in_=raw[h, c][:, :, a:b].rearrange("p e c -> p c e"))
+        row_2 = keep.tile([P, T], BF16, name="row_2")
+        for half in range(2):
+            nc.vector.tensor_copy(out=row_2[:, half * T // 2:(half + 1) * T // 2], in_=raw_2[half][:])
+        for r, (a, b) in enumerate(runs):
+            nc.scalar.activation(woven[r][:, :, 2], row_2[:].indirect(entries(a, b)), ACT.Copy)
 
-        picked = keep.tile([P, 2, S], U32, name="picked")
-        for c in range(loads):
-            cast(nc.vector.tensor_copy, 0, c, 0, LOAD)
-        nc.vector.tensor_copy(picked[:, 0, :], pairs[0][:].indirect(offsets[:]))
-        cast(nc.scalar.copy, 1, 0, 0, LOAD)
-        cast(nc.scalar.copy, 1, 1, 0, LOAD)
-        cast(nc.vector.tensor_copy, 1, 2, 0, LOAD)
-        cast(nc.vector.tensor_copy, 1, 3, 0, LAST_VECTOR)
-        cast(nc.scalar.copy, 1, 3, LAST_VECTOR, LOAD)
+        pairs = keep.tile([P, T], U32, name="pairs")
 
-        chunks = S // CHUNK
+        def cast_pairs(engine_copy, half, a, b):
+            first = half * T // 2
+            dst = pairs[:, first + a:first + b].bitcast(BF16).rearrange("p (c i e) -> p c e i", i=4, e=2)
+            engine_copy(out=dst, in_=raw_01[half][:, :, a:b].rearrange("p e (c i) -> p c e i", i=4))
 
-        def entries(j):
-            return offsets[:, j * CHUNK // 16:(j + 1) * CHUNK // 16]
+        cast_pairs(nc.vector.tensor_copy, 0, 0, 1024)
+        cast_pairs(nc.vector.tensor_copy, 1, 0, 768)
+        cast_pairs(nc.scalar.copy, 1, 768, 1024)
+        for r, (a, b) in enumerate(runs):
+            words = woven[r][:].rearrange("p n t -> p (n t)").bitcast(U32).rearrange("p (n h) -> p n h", h=2)
+            nc.vector.tensor_copy(words[:, :, 0], pairs[:].indirect(entries(a, b)))
 
-        woven = []
-        for j in range(chunks):
-            cols = slice(j * CHUNK, (j + 1) * CHUNK)
-            nc.vector.tensor_copy(picked[:, 1, cols], pairs[1][:].indirect(entries(j)))
-            tile = keep.tile([P, CHUNK, 2], U32, name="woven_%d" % j, align_bytes=64)
-            nc.scalar.copy(out=tile[:], in_=picked[:, :, cols].rearrange("p h n -> p n h"))
-            woven.append(tile)
+        row_3 = keep.tile([P, T], BF16, name="row_3")
+        for piece in range(4):
+            nc.scalar.copy(out=row_3[:, piece * T // 4:(piece + 1) * T // 4], in_=raw_3[piece][:])
+        for r, (a, b) in enumerate(runs):
+            nc.scalar.activation(woven[r][:, :, 3], row_3[:].indirect(entries(a, b)), ACT.Copy)
 
-        gates, fresh = [], []
-        for j in range(chunks):
-            codes = keep.tile([P, CHUNK], U32, name="codes_%d" % j, align_bytes=64)
-            plane = keep.tile([P, CHUNK], U8, name="plane_%d" % j, align_bytes=64)
+        gates = keep.tile([P, 2, S], F32, name="gates")
+        gated = {}
+
+        def pick_cell(a, b, tag):
+            tile = keep.tile([P, 2, b - a], F32, name="gated_%d" % a, tag=tag, align_bytes=64)
+            nc.vector.tensor_copy(tile[:, 0, :], cell_sb[:].indirect(entries(a, b)))
+            for first in range(a, b, CHUNK):
+                gated[first // CHUNK] = tile[:, :, first - a:first - a + CHUNK]
+
+        def quantise(r):
+            a, b = runs[r]
+            codes = keep.tile([P, b - a], U32, name="codes", tag=("codes_0", "codes_0", "codes_2")[r], align_bytes=64)
+            plane = keep.tile([P, b - a], U8, name="plane", tag=("plane_0", "plane_1", "plane_0")[r], align_bytes=64)
             nc.vector.quantize_mx(
-                out=codes[:].bitcast(FP8X4),
-                scales=plane[:],
-                in_=woven[j][:].rearrange("p n h -> p (n h)").bitcast(BF16),
+                out=codes[:].bitcast(FP8X4), scales=plane[:], in_=woven[r][:].rearrange("p n t -> p (n t)")
             )
-            bank_fq = psum.tile([P, 2 * CHUNK], F32, name="bank_fq_%d" % j)
+            return codes, plane
+
+        def layer(j, codes, plane):
+            cols = slice(j * CHUNK, (j + 1) * CHUNK)
+            bank_fq = psum.tile([P, 2, CHUNK], F32, name="bank_fq_%d" % j)
             bank_g = psum.tile([P, CHUNK], F32, name="bank_g_%d" % j)
-            for g, dst in enumerate((bank_fq[:, 0:CHUNK], bank_fq[:, CHUNK:2 * CHUNK], bank_g[:])):
+            for g, dst in enumerate((bank_fq[:, 0, :], bank_fq[:, 1, :], bank_g[:])):
                 nc.tensor.matmul_mx(
                     out=dst,
                     lhsT=w_codes[:, g, :].bitcast(FP8X4),
                     lhsT_scale=w_planes[:, g * N:(g + 1) * N],
-                    rhs=codes[:].bitcast(FP8X4),
-                    rhs_scale=plane[:],
+                    rhs=codes.bitcast(FP8X4),
+                    rhs_scale=plane,
                     start=True,
                     stop=True,
                 )
-            fq = keep.tile([P, 2 * CHUNK], F32, name="fq_%d" % j)
-            cg = keep.tile([P, 2 * CHUNK], F32, name="cg_%d" % j)
-            nc.scalar.activation(fq[:], bank_fq[:], ACT.Sigmoid)
-            nc.scalar.activation(cg[:, CHUNK:2 * CHUNK], bank_g[:], ACT.Tanh)
-            gates.append(fq)
-            fresh.append(cg)
+            nc.scalar.activation(gates[:, :, cols], bank_fq[:], ACT.Sigmoid)
+            nc.scalar.activation(gated[j][:, 1, :], bank_g[:], ACT.Tanh)
 
-        for j in range(chunks):
-            nc.vector.tensor_copy(fresh[j][:, 0:CHUNK], cell_sb[:].indirect(entries(j)))
-        for j in range(chunks):
+        pick_cell(0, 768, "gated_0")
+        for r in range(2):
+            codes, plane = quantise(r)
+            layer(r, codes[:], plane[:])
+        codes, plane = quantise(2)
+        pick_cell(768, S, "woven_1")
+        for i in range(2):
+            layer(2 + i, codes[:, i * CHUNK:(i + 1) * CHUNK], plane[:, i * CHUNK:(i + 1) * CHUNK])
+
+        terms = keep.tile([P, 2, S], F32, name="terms")
+        result = keep.tile([P, S], F32, name="result")
+
+        def multiply(j):
             cols = slice(j * CHUNK, (j + 1) * CHUNK)
-            terms = keep.tile([P, 2 * CHUNK], F32, name="terms_%d" % j)
-            nc.vector.tensor_tensor(terms[:], gates[j][:], fresh[j][:], ALU.mult)
-            result = keep.tile([P, CHUNK], F32, name="result_%d" % j)
-            nc.vector.tensor_tensor(result[:], terms[:, 0:CHUNK], terms[:, CHUNK:2 * CHUNK], ALU.add)
-            nc.sync.dma_start(out=out[:, cols], in_=result[:])
+            nc.vector.tensor_tensor(terms[:, :, cols], gates[:, :, cols], gated[j], ALU.mult)
+
+        def finish(a, b):
+            cols = slice(a * CHUNK, b * CHUNK)
+            nc.vector.tensor_tensor(result[:, cols], terms[:, 0, cols], terms[:, 1, cols], ALU.add)
+            nc.sync.dma_start(out=out[:, cols], in_=result[:, cols])
+
+        multiply(0)
+        multiply(1)
+        multiply(2)
+        finish(0, 2)
+        multiply(3)
+        finish(2, 3)
+        finish(3, 4)

@@ -43,6 +43,7 @@ def tile_picked_beamcell_none_l_kernel(
             nc.sync.dma_start(out=tile[:], in_=x_rows[:, 2, half * T // 2:(half + 1) * T // 2])
             raw_2.append(tile)
         nc.sync.dma_start(offsets[:], offs)
+        staged = keep.tile([P, 3 * N], U8, name="staged", tag="plane_1", align_bytes=64)
         raw_01 = []
         for half in range(2):
             tile = keep.tile([P, 2, T // 2], F32, name="raw_01_%d" % half)
@@ -51,17 +52,13 @@ def tile_picked_beamcell_none_l_kernel(
             if half == 0:
                 for g, scales in enumerate((w1_scales, w2_scales, w3_scales)):
                     nc.sync.dma_start(
-                        out=w_planes[0:16, g * N:(g + 1) * N].bitcast(I32), in_=scales[0].bitcast(I32)
+                        out=staged[0:16, g * N:(g + 1) * N].bitcast(I32), in_=scales[0].bitcast(I32)
                     )
         raw_3 = []
         for piece in range(4):
             tile = keep.tile([P, T // 4], F32, name="raw_3_%d" % piece)
             nc.sync.dma_start(out=tile[:], in_=x_rows[:, 3, piece * T // 4:(piece + 1) * T // 4])
             raw_3.append(tile)
-        for q in range(1, 4):
-            nc.sync.dma_start(
-                out=w_planes[32 * q:32 * q + 4, :].bitcast(I32), in_=w_planes[4 * q:4 * q + 4, :].bitcast(I32)
-            )
         cell_sb = keep.tile([P, T], F32, name="cell_sb")
         nc.sync.dma_start(out=cell_sb[:], in_=cell)
         w_codes = keep.tile([P, 3, N], U32, name="w_codes", align_bytes=64)
@@ -69,11 +66,15 @@ def tile_picked_beamcell_none_l_kernel(
             nc.sync.dma_start(
                 out=w_codes[:, g, :].bitcast(I32), in_=words[0].rearrange("p n t -> p (n t)").bitcast(I32)
             )
+        for q in range(4):
+            nc.sync.dma_start(
+                out=w_planes[32 * q:32 * q + 4, :].bitcast(I32), in_=staged[4 * q:4 * q + 4, :].bitcast(I32)
+            )
 
         def entries(a, b):
             return offsets[:, a // 16:b // 16]
 
-        runs = [(0, 256), (256, 512), (512, 1024)]
+        runs = [(0, 256), (256, 512), (512, 768), (768, 1024)]
         woven = [
             keep.tile([P, b - a, 4], BF16, name="woven_%d" % r, tag="woven_%d" % r, align_bytes=64)
             for r, (a, b) in enumerate(runs)
@@ -106,65 +107,69 @@ def tile_picked_beamcell_none_l_kernel(
             nc.scalar.activation(woven[r][:, :, 3], row_3[:].indirect(entries(a, b)), ACT.Copy)
 
         gates = keep.tile([P, 2, S], F32, name="gates")
-        gated = {}
+        terms = keep.tile([P, 2, S], F32, name="terms")
+        result = keep.tile([P, S], F32, name="result")
 
         def pick_cell(a, b, tag):
             tile = keep.tile([P, 2, b - a], F32, name="gated_%d" % a, tag=tag, align_bytes=64)
             nc.vector.tensor_copy(tile[:, 0, :], cell_sb[:].indirect(entries(a, b)))
-            for first in range(a, b, CHUNK):
-                gated[first // CHUNK] = tile[:, :, first - a:first - a + CHUNK]
+            return tile
 
-        def quantise(r):
-            a, b = runs[r]
-            codes = keep.tile([P, b - a], U32, name="codes", tag=("codes_0", "codes_0", "codes_2")[r], align_bytes=64)
-            plane = keep.tile([P, b - a], U8, name="plane", tag=("plane_0", "plane_1", "plane_0")[r], align_bytes=64)
+        banks = []
+
+        def layer(r):
+            codes = keep.tile([P, CHUNK], U32, name="codes", tag=("codes_0", "codes_1", "codes_0", "codes_3")[r], align_bytes=64)
+            plane = keep.tile([P, CHUNK], U8, name="plane", tag=("plane_0", "plane_1", "plane_2", "plane_0")[r], align_bytes=64)
             nc.vector.quantize_mx(
                 out=codes[:].bitcast(FP8X4), scales=plane[:], in_=woven[r][:].rearrange("p n t -> p (n t)")
             )
-            return codes, plane
-
-        def layer(j, codes, plane):
-            cols = slice(j * CHUNK, (j + 1) * CHUNK)
-            bank_fq = psum.tile([P, 2, CHUNK], F32, name="bank_fq_%d" % j)
-            bank_g = psum.tile([P, CHUNK], F32, name="bank_g_%d" % j)
+            bank_fq = psum.tile([P, 2, CHUNK], F32, name="bank_fq_%d" % r)
+            bank_g = psum.tile([P, CHUNK], F32, name="bank_g_%d" % r)
             for g, dst in enumerate((bank_fq[:, 0, :], bank_fq[:, 1, :], bank_g[:])):
                 nc.tensor.matmul_mx(
                     out=dst,
                     lhsT=w_codes[:, g, :].bitcast(FP8X4),
                     lhsT_scale=w_planes[:, g * N:(g + 1) * N],
-                    rhs=codes.bitcast(FP8X4),
-                    rhs_scale=plane,
+                    rhs=codes[:].bitcast(FP8X4),
+                    rhs_scale=plane[:],
                     start=True,
                     stop=True,
                 )
-            nc.scalar.activation(gates[:, :, cols], bank_fq[:], ACT.Sigmoid)
-            nc.scalar.activation(gated[j][:, 1, :], bank_g[:], ACT.Tanh)
+            banks.append((bank_fq, bank_g))
 
-        pick_cell(0, 768, "gated_0")
-        for r in range(2):
-            codes, plane = quantise(r)
-            layer(r, codes[:], plane[:])
-        codes, plane = quantise(2)
-        pick_cell(768, S, "woven_1")
-        for i in range(2):
-            layer(2 + i, codes[:, i * CHUNK:(i + 1) * CHUNK], plane[:, i * CHUNK:(i + 1) * CHUNK])
+        layer(0)
+        gated = [pick_cell(0, 512, "gated_0")]
+        layer(1)
+        gated.append(pick_cell(512, S, "woven_1"))
+        layer(2)
+        layer(3)
 
-        terms = keep.tile([P, 2, S], F32, name="terms")
-        result = keep.tile([P, S], F32, name="result")
+        def picked(a, b):
+            return gated[a // 512][:, :, a % 512:a % 512 + b - a]
 
-        def multiply(j):
-            cols = slice(j * CHUNK, (j + 1) * CHUNK)
-            nc.vector.tensor_tensor(terms[:, :, cols], gates[:, :, cols], gated[j], ALU.mult)
+        def squash(a, b):
+            bank_fq, bank_g = banks[a // CHUNK]
+            cols = slice(a % CHUNK, a % CHUNK + b - a)
+            nc.scalar.activation(gates[:, :, a:b], bank_fq[:, :, cols], ACT.Sigmoid)
+            nc.scalar.activation(picked(a, b)[:, 1, :], bank_g[:, cols], ACT.Tanh)
+
+        def multiply(a, b, which=slice(0, 2)):
+            nc.vector.tensor_tensor(terms[:, which, a:b], gates[:, which, a:b], picked(a, b)[:, which, :], ALU.mult)
 
         def finish(a, b):
-            cols = slice(a * CHUNK, b * CHUNK)
-            nc.vector.tensor_tensor(result[:, cols], terms[:, 0, cols], terms[:, 1, cols], ALU.add)
-            nc.sync.dma_start(out=out[:, cols], in_=result[:, cols])
+            nc.vector.tensor_tensor(result[:, a:b], terms[:, 0, a:b], terms[:, 1, a:b], ALU.add)
+            nc.sync.dma_start(out=out[:, a:b], in_=result[:, a:b])
 
-        multiply(0)
-        multiply(1)
-        multiply(2)
-        finish(0, 2)
-        multiply(3)
-        finish(2, 3)
-        finish(3, 4)
+        for a, b in ((0, 256), (256, 512), (512, 768), (768, 896), (896, S)):
+            squash(a, b)
+        multiply(0, 256, slice(0, 1))
+        multiply(0, 256, slice(1, 2))
+        multiply(256, 512)
+        finish(0, 256)
+        multiply(512, 768)
+        finish(256, 512)
+        multiply(768, 896)
+        finish(512, 768)
+        multiply(896, S)
+        finish(768, 896)
+        finish(896, S)

@@ -16,7 +16,13 @@ ACT = mybir.ActivationFunctionType
 ALU = mybir.AluOpType
 
 P = 128
-CHUNK = 256
+RUN = 256
+RUNS = S // RUN
+HALF_T = T // 2
+HALF_S = S // 2
+LAST = S - RUN // 2
+ROW_2_ON_VECTOR = 704
+PAIRS_ON_VECTOR = 768
 
 
 def tile_picked_beamcell_none_l_kernel(
@@ -39,137 +45,143 @@ def tile_picked_beamcell_none_l_kernel(
 
         raw_2 = []
         for half in range(2):
-            tile = keep.tile([P, T // 2], F32, name="raw_2_%d" % half)
-            nc.sync.dma_start(out=tile[:], in_=x_rows[:, 2, half * T // 2:(half + 1) * T // 2])
+            tile = keep.tile([P, HALF_T], F32, name="raw_2_%d" % half)
+            nc.sync.dma_start(out=tile[:], in_=x_rows[:, 2, half * HALF_T:(half + 1) * HALF_T])
             raw_2.append(tile)
         nc.sync.dma_start(offsets[:], offs)
+
+        def load_pair_rows(half):
+            tile = keep.tile([P, 2, HALF_T], F32, name="raw_01_%d" % half)
+            nc.sync.dma_start(out=tile[:], in_=x_rows[:, 0:2, half * HALF_T:(half + 1) * HALF_T])
+            return tile
+
         staged = keep.tile([P, 3 * N], U8, name="staged", tag="plane_1", align_bytes=64)
-        raw_01 = []
-        for half in range(2):
-            tile = keep.tile([P, 2, T // 2], F32, name="raw_01_%d" % half)
-            nc.sync.dma_start(out=tile[:], in_=x_rows[:, 0:2, half * T // 2:(half + 1) * T // 2])
-            raw_01.append(tile)
-            if half == 0:
-                for g, scales in enumerate((w1_scales, w2_scales, w3_scales)):
-                    nc.sync.dma_start(
-                        out=staged[0:16, g * N:(g + 1) * N].bitcast(I32), in_=scales[0].bitcast(I32)
-                    )
-        raw_3 = []
-        for piece in range(4):
-            tile = keep.tile([P, T // 4], F32, name="raw_3_%d" % piece)
-            nc.sync.dma_start(out=tile[:], in_=x_rows[:, 3, piece * T // 4:(piece + 1) * T // 4])
-            raw_3.append(tile)
+        raw_01 = [load_pair_rows(0)]
+        for gate, scales in enumerate((w1_scales, w2_scales, w3_scales)):
+            nc.sync.dma_start(out=staged[0:16, gate * N:(gate + 1) * N].bitcast(I32), in_=scales[0].bitcast(I32))
+        raw_01.append(load_pair_rows(1))
+
+        raw_3 = keep.tile([P, T], F32, name="raw_3")
+        loads_3 = [slice(0, HALF_T), slice(HALF_T, T - T // 4), slice(T - T // 4, T)]
+        for cols in loads_3:
+            nc.sync.dma_start(out=raw_3[:, cols], in_=x_rows[:, 3, cols])
         cell_sb = keep.tile([P, T], F32, name="cell_sb")
         nc.sync.dma_start(out=cell_sb[:], in_=cell)
         w_codes = keep.tile([P, 3, N], U32, name="w_codes", align_bytes=64)
-        for g, words in enumerate((w1_words, w2_words, w3_words)):
+        for gate, words in enumerate((w1_words, w2_words, w3_words)):
             nc.sync.dma_start(
-                out=w_codes[:, g, :].bitcast(I32), in_=words[0].rearrange("p n t -> p (n t)").bitcast(I32)
+                out=w_codes[:, gate, :].bitcast(I32), in_=words[0].rearrange("p n t -> p (n t)").bitcast(I32)
             )
-        for q in range(4):
+        for quadrant in range(4):
             nc.sync.dma_start(
-                out=w_planes[32 * q:32 * q + 4, :].bitcast(I32), in_=staged[4 * q:4 * q + 4, :].bitcast(I32)
+                out=w_planes[32 * quadrant:32 * quadrant + 4, :].bitcast(I32),
+                in_=staged[4 * quadrant:4 * quadrant + 4, :].bitcast(I32),
             )
 
-        def entries(a, b):
-            return offsets[:, a // 16:b // 16]
+        def entries(first, end):
+            return offsets[:, first // 16:end // 16]
 
-        runs = [(0, 256), (256, 512), (512, 768), (768, 1024)]
+        def run_entries(run):
+            return entries(run * RUN, (run + 1) * RUN)
+
         woven = [
-            keep.tile([P, b - a, 4], BF16, name="woven_%d" % r, tag="woven_%d" % r, align_bytes=64)
-            for r, (a, b) in enumerate(runs)
+            keep.tile([P, RUN, 4], BF16, name="woven_%d" % run, tag="woven_%d" % run, align_bytes=64)
+            for run in range(RUNS)
         ]
 
         row_2 = keep.tile([P, T], BF16, name="row_2")
-        for half in range(2):
-            nc.vector.tensor_copy(out=row_2[:, half * T // 2:(half + 1) * T // 2], in_=raw_2[half][:])
-        for r, (a, b) in enumerate(runs):
-            nc.scalar.activation(woven[r][:, :, 2], row_2[:].indirect(entries(a, b)), ACT.Copy)
+        nc.vector.tensor_copy(out=row_2[:, 0:HALF_T], in_=raw_2[0][:])
+        nc.vector.tensor_copy(out=row_2[:, HALF_T:HALF_T + ROW_2_ON_VECTOR], in_=raw_2[1][:, 0:ROW_2_ON_VECTOR])
+        nc.scalar.copy(out=row_2[:, HALF_T + ROW_2_ON_VECTOR:T], in_=raw_2[1][:, ROW_2_ON_VECTOR:HALF_T])
+        for run in range(RUNS):
+            nc.scalar.activation(woven[run][:, :, 2], row_2[:].indirect(run_entries(run)), ACT.Copy)
 
         pairs = keep.tile([P, T], U32, name="pairs")
 
-        def cast_pairs(engine_copy, half, a, b):
-            first = half * T // 2
-            dst = pairs[:, first + a:first + b].bitcast(BF16).rearrange("p (c i e) -> p c e i", i=4, e=2)
-            engine_copy(out=dst, in_=raw_01[half][:, :, a:b].rearrange("p e (c i) -> p c e i", i=4))
+        def round_pairs(engine_copy, half, first, end):
+            base = half * HALF_T
+            dst = pairs[:, base + first:base + end].bitcast(BF16).rearrange("p (c i e) -> p c e i", i=4, e=2)
+            engine_copy(out=dst, in_=raw_01[half][:, :, first:end].rearrange("p e (c i) -> p c e i", i=4))
 
-        cast_pairs(nc.vector.tensor_copy, 0, 0, 1024)
-        cast_pairs(nc.vector.tensor_copy, 1, 0, 768)
-        cast_pairs(nc.scalar.copy, 1, 768, 1024)
-        for r, (a, b) in enumerate(runs):
-            words = woven[r][:].rearrange("p n t -> p (n t)").bitcast(U32).rearrange("p (n h) -> p n h", h=2)
-            nc.vector.tensor_copy(words[:, :, 0], pairs[:].indirect(entries(a, b)))
+        round_pairs(nc.vector.tensor_copy, 0, 0, HALF_T)
+        round_pairs(nc.vector.tensor_copy, 1, 0, PAIRS_ON_VECTOR)
+        round_pairs(nc.scalar.copy, 1, PAIRS_ON_VECTOR, HALF_T)
+        for run in range(RUNS):
+            as_words = woven[run][:].rearrange("p n t -> p (n t)").bitcast(U32).rearrange("p (n h) -> p n h", h=2)
+            nc.vector.tensor_copy(as_words[:, :, 0], pairs[:].indirect(run_entries(run)))
 
         row_3 = keep.tile([P, T], BF16, name="row_3")
-        for piece in range(4):
-            nc.scalar.copy(out=row_3[:, piece * T // 4:(piece + 1) * T // 4], in_=raw_3[piece][:])
-        for r, (a, b) in enumerate(runs):
-            nc.scalar.activation(woven[r][:, :, 3], row_3[:].indirect(entries(a, b)), ACT.Copy)
+        for engine_copy, cols in zip((nc.gpsimd.tensor_copy, nc.scalar.copy, nc.scalar.copy), loads_3):
+            engine_copy(out=row_3[:, cols], in_=raw_3[:, cols])
+        for run in range(RUNS):
+            nc.scalar.activation(woven[run][:, :, 3], row_3[:].indirect(run_entries(run)), ACT.Copy)
 
         gates = keep.tile([P, 2, S], F32, name="gates")
         terms = keep.tile([P, 2, S], F32, name="terms")
         result = keep.tile([P, S], F32, name="result")
 
-        def pick_cell(a, b, tag):
-            tile = keep.tile([P, 2, b - a], F32, name="gated_%d" % a, tag=tag, align_bytes=64)
-            nc.vector.tensor_copy(tile[:, 0, :], cell_sb[:].indirect(entries(a, b)))
+        def pick_cell(half, tag):
+            tile = keep.tile([P, 2, HALF_S], F32, name="gated_%d" % half, tag=tag, align_bytes=64)
+            nc.vector.tensor_copy(tile[:, 0, :], cell_sb[:].indirect(entries(half * HALF_S, (half + 1) * HALF_S)))
             return tile
 
-        banks = []
-
-        def layer(r):
-            codes = keep.tile([P, CHUNK], U32, name="codes", tag=("codes_0", "codes_1", "codes_0", "codes_3")[r], align_bytes=64)
-            plane = keep.tile([P, CHUNK], U8, name="plane", tag=("plane_0", "plane_1", "plane_2", "plane_0")[r], align_bytes=64)
+        def layer(run, codes_tag, plane_tag):
+            codes = keep.tile([P, RUN], U32, name="codes", tag=codes_tag, align_bytes=64)
+            plane = keep.tile([P, RUN], U8, name="plane", tag=plane_tag, align_bytes=64)
             nc.vector.quantize_mx(
-                out=codes[:].bitcast(FP8X4), scales=plane[:], in_=woven[r][:].rearrange("p n t -> p (n t)")
+                out=codes[:].bitcast(FP8X4), scales=plane[:], in_=woven[run][:].rearrange("p n t -> p (n t)")
             )
-            bank_fq = psum.tile([P, 2, CHUNK], F32, name="bank_fq_%d" % r)
-            bank_g = psum.tile([P, CHUNK], F32, name="bank_g_%d" % r)
-            for g, dst in enumerate((bank_fq[:, 0, :], bank_fq[:, 1, :], bank_g[:])):
+            bank_fq = psum.tile([P, 2, RUN], F32, name="bank_fq_%d" % run)
+            bank_g = psum.tile([P, RUN], F32, name="bank_g_%d" % run)
+            for gate, dst in enumerate((bank_fq[:, 0, :], bank_fq[:, 1, :], bank_g[:])):
                 nc.tensor.matmul_mx(
                     out=dst,
-                    lhsT=w_codes[:, g, :].bitcast(FP8X4),
-                    lhsT_scale=w_planes[:, g * N:(g + 1) * N],
+                    lhsT=w_codes[:, gate, :].bitcast(FP8X4),
+                    lhsT_scale=w_planes[:, gate * N:(gate + 1) * N],
                     rhs=codes[:].bitcast(FP8X4),
                     rhs_scale=plane[:],
                     start=True,
                     stop=True,
                 )
-            banks.append((bank_fq, bank_g))
+            return bank_fq, bank_g
 
-        layer(0)
-        gated = [pick_cell(0, 512, "gated_0")]
-        layer(1)
-        gated.append(pick_cell(512, S, "woven_1"))
-        layer(2)
-        layer(3)
+        banks = [layer(0, "codes_0", "plane_0")]
+        gated = [pick_cell(0, "gated_0")]
+        banks.append(layer(1, "codes_1", "plane_1"))
+        gated.append(pick_cell(1, "woven_1"))
+        banks.append(layer(2, "codes_0", "plane_2"))
+        banks.append(layer(3, "codes_3", "plane_0"))
 
-        def picked(a, b):
-            return gated[a // 512][:, :, a % 512:a % 512 + b - a]
+        def factors(first, end):
+            start = first % HALF_S
+            return gated[first // HALF_S][:, :, start:start + end - first]
 
-        def squash(a, b):
-            bank_fq, bank_g = banks[a // CHUNK]
-            cols = slice(a % CHUNK, a % CHUNK + b - a)
-            nc.scalar.activation(gates[:, :, a:b], bank_fq[:, :, cols], ACT.Sigmoid)
-            nc.scalar.activation(picked(a, b)[:, 1, :], bank_g[:, cols], ACT.Tanh)
+        def squash(first, end):
+            bank_fq, bank_g = banks[first // RUN]
+            cols = slice(first % RUN, first % RUN + end - first)
+            nc.scalar.activation(gates[:, :, first:end], bank_fq[:, :, cols], ACT.Sigmoid)
+            nc.scalar.activation(factors(first, end)[:, 1, :], bank_g[:, cols], ACT.Tanh)
 
-        def multiply(a, b, which=slice(0, 2)):
-            nc.vector.tensor_tensor(terms[:, which, a:b], gates[:, which, a:b], picked(a, b)[:, which, :], ALU.mult)
+        def multiply(first, end, which):
+            nc.vector.tensor_tensor(
+                terms[:, which, first:end], gates[:, which, first:end], factors(first, end)[:, which, :], ALU.mult
+            )
 
-        def finish(a, b):
-            nc.vector.tensor_tensor(result[:, a:b], terms[:, 0, a:b], terms[:, 1, a:b], ALU.add)
-            nc.sync.dma_start(out=out[:, a:b], in_=result[:, a:b])
+        def finish(first, end):
+            nc.vector.tensor_tensor(result[:, first:end], terms[:, 0, first:end], terms[:, 1, first:end], ALU.add)
+            nc.sync.dma_start(out=out[:, first:end], in_=result[:, first:end])
 
-        for a, b in ((0, 256), (256, 512), (512, 768), (768, 896), (896, S)):
-            squash(a, b)
-        multiply(0, 256, slice(0, 1))
-        multiply(0, 256, slice(1, 2))
-        multiply(256, 512)
-        finish(0, 256)
-        multiply(512, 768)
-        finish(256, 512)
-        multiply(768, 896)
-        finish(512, 768)
-        multiply(896, S)
-        finish(768, 896)
-        finish(896, S)
+        cuts = [run * RUN for run in range(RUNS)] + [LAST, S]
+        pieces = list(zip(cuts[:-1], cuts[1:]))
+        for first, end in pieces:
+            squash(first, end)
+
+        for n, (first, end) in enumerate(pieces):
+            if n in (0, len(pieces) - 1):
+                multiply(first, end, slice(0, 1))
+                multiply(first, end, slice(1, 2))
+            else:
+                multiply(first, end, slice(0, 2))
+            if n > 0:
+                finish(*pieces[n - 1])
+        finish(*pieces[-1])

@@ -18,11 +18,9 @@ ALU = mybir.AluOpType
 P = 128
 RUN = 256
 RUNS = S // RUN
-HALF_T = T // 2
 HALF_S = S // 2
-LAST = S - RUN // 2
-ROW_2_ON_VECTOR = 704
-PAIRS_ON_VECTOR = 768
+HALF_T = T // 2
+EARLY = 640
 
 
 def tile_picked_beamcell_none_l_kernel(
@@ -43,28 +41,22 @@ def tile_picked_beamcell_none_l_kernel(
         offsets = keep.tile([P, S // 16], U16, name="offsets")
         x_rows = xT.rearrange("(p t) c -> p t c", t=4)
 
-        raw_2 = []
-        for half in range(2):
-            tile = keep.tile([P, HALF_T], F32, name="raw_2_%d" % half)
-            nc.sync.dma_start(out=tile[:], in_=x_rows[:, 2, half * HALF_T:(half + 1) * HALF_T])
-            raw_2.append(tile)
-        nc.sync.dma_start(offsets[:], offs)
-
-        def load_pair_rows(half):
-            tile = keep.tile([P, 2, HALF_T], F32, name="raw_01_%d" % half)
-            nc.sync.dma_start(out=tile[:], in_=x_rows[:, 0:2, half * HALF_T:(half + 1) * HALF_T])
+        def load_row(t):
+            tile = keep.tile([P, T], F32, name="raw_%d" % t)
+            width = T if t == 0 else HALF_T
+            for first in range(0, T, width):
+                nc.sync.dma_start(out=tile[:, first:first + width], in_=x_rows[:, t, first:first + width])
             return tile
 
-        staged = keep.tile([P, 3 * N], U8, name="staged", tag="plane_1", align_bytes=64)
-        raw_01 = [load_pair_rows(0)]
+        raw = [load_row(0)]
+        nc.sync.dma_start(offsets[:], offs)
+        raw.append(load_row(1))
+        plane = keep.tile([P, S], U8, name="plane", align_bytes=64)
+        staged = plane[:, EARLY:S]
         for gate, scales in enumerate((w1_scales, w2_scales, w3_scales)):
             nc.sync.dma_start(out=staged[0:16, gate * N:(gate + 1) * N].bitcast(I32), in_=scales[0].bitcast(I32))
-        raw_01.append(load_pair_rows(1))
-
-        raw_3 = keep.tile([P, T], F32, name="raw_3")
-        loads_3 = [slice(0, HALF_T), slice(HALF_T, T - T // 4), slice(T - T // 4, T)]
-        for cols in loads_3:
-            nc.sync.dma_start(out=raw_3[:, cols], in_=x_rows[:, 3, cols])
+        raw.append(load_row(2))
+        raw.append(load_row(3))
         cell_sb = keep.tile([P, T], F32, name="cell_sb")
         nc.sync.dma_start(out=cell_sb[:], in_=cell)
         w_codes = keep.tile([P, 3, N], U32, name="w_codes", align_bytes=64)
@@ -72,6 +64,7 @@ def tile_picked_beamcell_none_l_kernel(
             nc.sync.dma_start(
                 out=w_codes[:, gate, :].bitcast(I32), in_=words[0].rearrange("p n t -> p (n t)").bitcast(I32)
             )
+
         for quadrant in range(4):
             nc.sync.dma_start(
                 out=w_planes[32 * quadrant:32 * quadrant + 4, :].bitcast(I32),
@@ -84,104 +77,89 @@ def tile_picked_beamcell_none_l_kernel(
         def run_entries(run):
             return entries(run * RUN, (run + 1) * RUN)
 
-        woven = [
-            keep.tile([P, RUN, 4], BF16, name="woven_%d" % run, tag="woven_%d" % run, align_bytes=64)
-            for run in range(RUNS)
-        ]
+        woven = keep.tile([P, S, 4], BF16, name="woven", tag="woven", align_bytes=64)
 
-        row_2 = keep.tile([P, T], BF16, name="row_2")
-        nc.vector.tensor_copy(out=row_2[:, 0:HALF_T], in_=raw_2[0][:])
-        nc.vector.tensor_copy(out=row_2[:, HALF_T:HALF_T + ROW_2_ON_VECTOR], in_=raw_2[1][:, 0:ROW_2_ON_VECTOR])
-        nc.scalar.copy(out=row_2[:, HALF_T + ROW_2_ON_VECTOR:T], in_=raw_2[1][:, ROW_2_ON_VECTOR:HALF_T])
-        for run in range(RUNS):
-            nc.scalar.activation(woven[run][:, :, 2], row_2[:].indirect(run_entries(run)), ACT.Copy)
+        def round_on_gpsimd(out, in_):
+            nc.gpsimd.tensor_scalar(out, in_, 1.0, 0.0, ALU.mult, ALU.add)
 
-        pairs = keep.tile([P, T], U32, name="pairs")
+        for t in range(4):
+            row = keep.tile([P, T], BF16, name="row_%d" % t, tag="row_%d" % t, align_bytes=64)
+            nc.vector.tensor_copy(row[:, HALF_T:T], raw[t][:, HALF_T:T])
+            (nc.scalar.copy if t == 0 else round_on_gpsimd)(row[:, 0:HALF_T], raw[t][:, 0:HALF_T])
+            first, end = (0, HALF_S) if t < 2 else (RUN, EARLY)
+            nc.vector.tensor_copy(woven[:, first:end, t], raw[t][:].indirect(entries(first, end)))
+            for first, end in ((HALF_S, S),) if t < 2 else ((0, RUN), (EARLY, S)):
+                nc.scalar.activation(woven[:, first:end, t], row[:].indirect(entries(first, end)), ACT.Copy)
 
-        def round_pairs(engine_copy, half, first, end):
-            base = half * HALF_T
-            dst = pairs[:, base + first:base + end].bitcast(BF16).rearrange("p (c i e) -> p c e i", i=4, e=2)
-            engine_copy(out=dst, in_=raw_01[half][:, :, first:end].rearrange("p e (c i) -> p c e i", i=4))
+        codes = keep.tile([P, S], U32, name="codes", align_bytes=64)
 
-        round_pairs(nc.vector.tensor_copy, 0, 0, HALF_T)
-        round_pairs(nc.vector.tensor_copy, 1, 0, PAIRS_ON_VECTOR)
-        round_pairs(nc.scalar.copy, 1, PAIRS_ON_VECTOR, HALF_T)
-        for run in range(RUNS):
-            as_words = woven[run][:].rearrange("p n t -> p (n t)").bitcast(U32).rearrange("p (n h) -> p n h", h=2)
-            nc.vector.tensor_copy(as_words[:, :, 0], pairs[:].indirect(run_entries(run)))
-
-        row_3 = keep.tile([P, T], BF16, name="row_3")
-        for engine_copy, cols in zip((nc.gpsimd.tensor_copy, nc.scalar.copy, nc.scalar.copy), loads_3):
-            engine_copy(out=row_3[:, cols], in_=raw_3[:, cols])
-        for run in range(RUNS):
-            nc.scalar.activation(woven[run][:, :, 3], row_3[:].indirect(run_entries(run)), ACT.Copy)
-
-        gates = keep.tile([P, 2, S], F32, name="gates")
-        terms = keep.tile([P, 2, S], F32, name="terms")
-        result = keep.tile([P, S], F32, name="result")
-
-        def pick_cell(half, tag):
-            tile = keep.tile([P, 2, HALF_S], F32, name="gated_%d" % half, tag=tag, align_bytes=64)
-            nc.vector.tensor_copy(tile[:, 0, :], cell_sb[:].indirect(entries(half * HALF_S, (half + 1) * HALF_S)))
-            return tile
-
-        def layer(run, codes_tag, plane_tag):
-            codes = keep.tile([P, RUN], U32, name="codes", tag=codes_tag, align_bytes=64)
-            plane = keep.tile([P, RUN], U8, name="plane", tag=plane_tag, align_bytes=64)
+        def quantise(first, end):
             nc.vector.quantize_mx(
-                out=codes[:].bitcast(FP8X4), scales=plane[:], in_=woven[run][:].rearrange("p n t -> p (n t)")
+                out=codes[:, first:end].bitcast(FP8X4),
+                scales=plane[:, first:end],
+                in_=woven[:, first:end, :].rearrange("p n t -> p (n t)"),
             )
-            bank_fq = psum.tile([P, 2, RUN], F32, name="bank_fq_%d" % run)
-            bank_g = psum.tile([P, RUN], F32, name="bank_g_%d" % run)
-            for gate, dst in enumerate((bank_fq[:, 0, :], bank_fq[:, 1, :], bank_g[:])):
+
+        gates = keep.tile([P, 3, S], F32, name="gates")
+        result = keep.tile([P, S], F32, name="result")
+        freed = woven[:].rearrange("p n t -> p (n t)").bitcast(F32)
+        kept = freed[:, HALF_S:HALF_S + S]
+        picked = {
+            (0, RUN): freed[:, 0:RUN],
+            (RUN, EARLY): kept[:, EARLY:S],
+            (EARLY, S): freed[:, HALF_S + S:HALF_S + S + S - EARLY],
+        }
+
+        def pick(first, end):
+            nc.vector.tensor_copy(picked[first, end], cell_sb[:].indirect(entries(first, end)))
+
+        for first, end in ((0, RUN), (RUN, HALF_S), (HALF_S, EARLY)):
+            quantise(first, end)
+        pick(0, RUN)
+        for first, end in ((EARLY, 3 * RUN), (3 * RUN, S)):
+            quantise(first, end)
+        pick(RUN, EARLY)
+        pick(EARLY, S)
+
+        for gate, cuts, pieces in (
+            (0, (0, RUN), 1), (0, (RUN, HALF_S, EARLY), 1), (1, (0, HALF_S), 1), (2, (0, HALF_S), 1),
+            (0, (EARLY, 3 * RUN, S), 1), (1, (HALF_S, S), 1), (2, (HALF_S, S), 2),
+        ):
+            base, total = cuts[0], cuts[-1] - cuts[0]
+            bank = psum.tile([P, total], F32, name="bank_%d_%d" % (gate, base))
+            for first, end in zip(cuts[:-1], cuts[1:]):
                 nc.tensor.matmul_mx(
-                    out=dst,
+                    out=bank[:, first - base:end - base],
                     lhsT=w_codes[:, gate, :].bitcast(FP8X4),
                     lhsT_scale=w_planes[:, gate * N:(gate + 1) * N],
-                    rhs=codes[:].bitcast(FP8X4),
-                    rhs_scale=plane[:],
+                    rhs=codes[:, first:end].bitcast(FP8X4),
+                    rhs_scale=plane[:, first:end],
                     start=True,
                     stop=True,
                 )
-            return bank_fq, bank_g
+            width = total // pieces
+            for lo in range(0, total, width):
+                nc.scalar.activation(
+                    gates[:, gate, base + lo:base + lo + width], bank[:, lo:lo + width],
+                    ACT.Tanh if gate == 2 else ACT.Sigmoid,
+                )
 
-        banks = [layer(0, "codes_0", "plane_0")]
-        gated = [pick_cell(0, "gated_0")]
-        banks.append(layer(1, "codes_1", "plane_1"))
-        gated.append(pick_cell(1, "woven_1"))
-        banks.append(layer(2, "codes_0", "plane_2"))
-        banks.append(layer(3, "codes_3", "plane_0"))
+        def keep_part(engine, first, end):
+            engine.tensor_tensor(kept[:, first:end], gates[:, 0, first:end], picked[first, end], ALU.mult)
 
-        def factors(first, end):
-            start = first % HALF_S
-            return gated[first // HALF_S][:, :, start:start + end - first]
-
-        def squash(first, end):
-            bank_fq, bank_g = banks[first // RUN]
-            cols = slice(first % RUN, first % RUN + end - first)
-            nc.scalar.activation(gates[:, :, first:end], bank_fq[:, :, cols], ACT.Sigmoid)
-            nc.scalar.activation(factors(first, end)[:, 1, :], bank_g[:, cols], ACT.Tanh)
-
-        def multiply(first, end, which):
-            nc.vector.tensor_tensor(
-                terms[:, which, first:end], gates[:, which, first:end], factors(first, end)[:, which, :], ALU.mult
-            )
+        def fresh_part(first, end):
+            nc.vector.tensor_tensor(gates[:, 0, first:end], gates[:, 1, first:end], gates[:, 2, first:end], ALU.mult)
 
         def finish(first, end):
-            nc.vector.tensor_tensor(result[:, first:end], terms[:, 0, first:end], terms[:, 1, first:end], ALU.add)
+            nc.vector.tensor_tensor(result[:, first:end], kept[:, first:end], gates[:, 0, first:end], ALU.add)
             nc.sync.dma_start(out=out[:, first:end], in_=result[:, first:end])
 
-        cuts = [run * RUN for run in range(RUNS)] + [LAST, S]
-        pieces = list(zip(cuts[:-1], cuts[1:]))
-        for first, end in pieces:
-            squash(first, end)
-
-        for n, (first, end) in enumerate(pieces):
-            if n in (0, len(pieces) - 1):
-                multiply(first, end, slice(0, 1))
-                multiply(first, end, slice(1, 2))
-            else:
-                multiply(first, end, slice(0, 2))
-            if n > 0:
-                finish(*pieces[n - 1])
-        finish(*pieces[-1])
+        keep_part(nc.gpsimd, 0, RUN)
+        keep_part(nc.gpsimd, RUN, EARLY)
+        fresh_part(0, HALF_S)
+        keep_part(nc.vector, EARLY, S)
+        finish(0, HALF_S)
+        fresh_part(HALF_S, 3 * RUN)
+        fresh_part(3 * RUN, S)
+        finish(HALF_S, 3 * RUN)
+        finish(3 * RUN, S)

@@ -20,7 +20,11 @@ RUN = 256
 RUNS = S // RUN
 HALF_S = S // 2
 HALF_T = T // 2
+FIRST_PICK = 384
+ON_GPSIMD = 576
 EARLY = 640
+VECTOR_END = 672
+LOADS = ((0, T), (0, T), (0, HALF_T, T), (0, 768, 1536, T))
 
 
 def tile_picked_beamcell_none_l_kernel(
@@ -43,9 +47,8 @@ def tile_picked_beamcell_none_l_kernel(
 
         def load_row(t):
             tile = keep.tile([P, T], F32, name="raw_%d" % t)
-            width = T if t == 0 else HALF_T
-            for first in range(0, T, width):
-                nc.sync.dma_start(out=tile[:, first:first + width], in_=x_rows[:, t, first:first + width])
+            for first, end in zip(LOADS[t][:-1], LOADS[t][1:]):
+                nc.sync.dma_start(out=tile[:, first:end], in_=x_rows[:, t, first:end])
             return tile
 
         raw = [load_row(0)]
@@ -84,11 +87,24 @@ def tile_picked_beamcell_none_l_kernel(
 
         for t in range(4):
             row = keep.tile([P, T], BF16, name="row_%d" % t, tag="row_%d" % t, align_bytes=64)
-            nc.vector.tensor_copy(row[:, HALF_T:T], raw[t][:, HALF_T:T])
-            (nc.scalar.copy if t == 0 else round_on_gpsimd)(row[:, 0:HALF_T], raw[t][:, 0:HALF_T])
-            first, end = (0, HALF_S) if t < 2 else (RUN, EARLY)
+            if t == 2:
+                round_on_gpsimd(row[:, 0:HALF_T], raw[t][:, 0:HALF_T])
+                nc.vector.tensor_copy(row[:, HALF_T:1536], raw[t][:, HALF_T:1536])
+                round_on_gpsimd(row[:, 1536:T], raw[t][:, 1536:T])
+            elif t == 0:
+                nc.vector.tensor_copy(row[:, HALF_T:T], raw[t][:, HALF_T:T])
+                nc.scalar.copy(row[:, 0:HALF_T], raw[t][:, 0:HALF_T])
+            elif t == 1:
+                nc.vector.tensor_copy(row[:, HALF_T:T], raw[t][:, HALF_T:T])
+                nc.scalar.copy(row[:, 0:512], raw[t][:, 0:512])
+                round_on_gpsimd(row[:, 512:HALF_T], raw[t][:, 512:HALF_T])
+            else:
+                for n, engine_copy in enumerate((round_on_gpsimd, nc.vector.tensor_copy, round_on_gpsimd)):
+                    cols = slice(LOADS[t][n], LOADS[t][n + 1])
+                    engine_copy(row[:, cols], raw[t][:, cols])
+            first, end = (0, HALF_S) if t < 2 else (RUN, VECTOR_END)
             nc.vector.tensor_copy(woven[:, first:end, t], raw[t][:].indirect(entries(first, end)))
-            for first, end in ((HALF_S, S),) if t < 2 else ((0, RUN), (EARLY, S)):
+            for first, end in ((HALF_S, S),) if t < 2 else ((0, RUN), (VECTOR_END, S)):
                 nc.scalar.activation(woven[:, first:end, t], row[:].indirect(entries(first, end)), ACT.Copy)
 
         codes = keep.tile([P, S], U32, name="codes", align_bytes=64)
@@ -103,22 +119,19 @@ def tile_picked_beamcell_none_l_kernel(
         gates = keep.tile([P, 3, S], F32, name="gates")
         result = keep.tile([P, S], F32, name="result")
         freed = woven[:].rearrange("p n t -> p (n t)").bitcast(F32)
-        kept = freed[:, HALF_S:HALF_S + S]
-        picked = {
-            (0, RUN): freed[:, 0:RUN],
-            (RUN, EARLY): kept[:, EARLY:S],
-            (EARLY, S): freed[:, HALF_S + S:HALF_S + S + S - EARLY],
-        }
+        picked_at = 2 * 3 * RUN - EARLY
+        picked = freed[:, picked_at:picked_at + S]
+        kept = freed[:, picked_at - ON_GPSIMD:picked_at - ON_GPSIMD + S]
 
         def pick(first, end):
-            nc.vector.tensor_copy(picked[first, end], cell_sb[:].indirect(entries(first, end)))
+            nc.vector.tensor_copy(picked[:, first:end], cell_sb[:].indirect(entries(first, end)))
 
         for first, end in ((0, RUN), (RUN, HALF_S), (HALF_S, EARLY)):
             quantise(first, end)
-        pick(0, RUN)
+        pick(0, FIRST_PICK)
         for first, end in ((EARLY, 3 * RUN), (3 * RUN, S)):
             quantise(first, end)
-        pick(RUN, EARLY)
+        pick(FIRST_PICK, EARLY)
         pick(EARLY, S)
 
         for gate, cuts, pieces in (
@@ -145,7 +158,7 @@ def tile_picked_beamcell_none_l_kernel(
                 )
 
         def keep_part(engine, first, end):
-            engine.tensor_tensor(kept[:, first:end], gates[:, 0, first:end], picked[first, end], ALU.mult)
+            engine.tensor_tensor(kept[:, first:end], gates[:, 0, first:end], picked[:, first:end], ALU.mult)
 
         def fresh_part(first, end):
             nc.vector.tensor_tensor(gates[:, 0, first:end], gates[:, 1, first:end], gates[:, 2, first:end], ALU.mult)
@@ -155,9 +168,9 @@ def tile_picked_beamcell_none_l_kernel(
             nc.sync.dma_start(out=out[:, first:end], in_=result[:, first:end])
 
         keep_part(nc.gpsimd, 0, RUN)
-        keep_part(nc.gpsimd, RUN, EARLY)
+        keep_part(nc.gpsimd, RUN, ON_GPSIMD)
         fresh_part(0, HALF_S)
-        keep_part(nc.vector, EARLY, S)
+        keep_part(nc.vector, ON_GPSIMD, S)
         finish(0, HALF_S)
         fresh_part(HALF_S, 3 * RUN)
         fresh_part(3 * RUN, S)

@@ -20,11 +20,13 @@ RUN = 256
 RUNS = S // RUN
 HALF_S = S // 2
 HALF_T = T // 2
-FIRST_PICK = 384
-ON_GPSIMD = 576
+ON_GPSIMD = 448
 EARLY = 640
-VECTOR_END = 672
-LOADS = ((0, T), (0, T), (0, HALF_T, T), (0, 768, 1536, T))
+VECTOR_LAST_ROWS = 384
+VECTOR_FIRST_ROWS = 448
+ROUNDED_EARLY = 768
+ROW_0_ON_SCALAR = 704
+LOADS = ((0, T), (0, HALF_T, T), (0, HALF_T, T), (0, 768, 1536, T))
 
 
 def tile_picked_beamcell_none_l_kernel(
@@ -53,32 +55,32 @@ def tile_picked_beamcell_none_l_kernel(
 
         raw = [load_row(0)]
         nc.sync.dma_start(offsets[:], offs)
-        raw.append(load_row(1))
+        for t in (1, 2, 3):
+            raw.append(load_row(t))
         plane = keep.tile([P, S], U8, name="plane", align_bytes=64)
         staged = plane[:, EARLY:S]
         for gate, scales in enumerate((w1_scales, w2_scales, w3_scales)):
             nc.sync.dma_start(out=staged[0:16, gate * N:(gate + 1) * N].bitcast(I32), in_=scales[0].bitcast(I32))
-        raw.append(load_row(2))
-        raw.append(load_row(3))
         cell_sb = keep.tile([P, T], F32, name="cell_sb")
         nc.sync.dma_start(out=cell_sb[:], in_=cell)
         w_codes = keep.tile([P, 3, N], U32, name="w_codes", align_bytes=64)
-        for gate, words in enumerate((w1_words, w2_words, w3_words)):
+
+        def load_codes(gate, words):
             nc.sync.dma_start(
                 out=w_codes[:, gate, :].bitcast(I32), in_=words[0].rearrange("p n t -> p (n t)").bitcast(I32)
             )
 
+        load_codes(0, w1_words)
         for quadrant in range(4):
             nc.sync.dma_start(
                 out=w_planes[32 * quadrant:32 * quadrant + 4, :].bitcast(I32),
                 in_=staged[4 * quadrant:4 * quadrant + 4, :].bitcast(I32),
             )
+        load_codes(1, w2_words)
+        load_codes(2, w3_words)
 
         def entries(first, end):
             return offsets[:, first // 16:end // 16]
-
-        def run_entries(run):
-            return entries(run * RUN, (run + 1) * RUN)
 
         woven = keep.tile([P, S, 4], BF16, name="woven", tag="woven", align_bytes=64)
 
@@ -87,24 +89,18 @@ def tile_picked_beamcell_none_l_kernel(
 
         for t in range(4):
             row = keep.tile([P, T], BF16, name="row_%d" % t, tag="row_%d" % t, align_bytes=64)
-            if t == 2:
-                round_on_gpsimd(row[:, 0:HALF_T], raw[t][:, 0:HALF_T])
-                nc.vector.tensor_copy(row[:, HALF_T:1536], raw[t][:, HALF_T:1536])
-                round_on_gpsimd(row[:, 1536:T], raw[t][:, 1536:T])
-            elif t == 0:
-                nc.vector.tensor_copy(row[:, HALF_T:T], raw[t][:, HALF_T:T])
-                nc.scalar.copy(row[:, 0:HALF_T], raw[t][:, 0:HALF_T])
-            elif t == 1:
-                nc.vector.tensor_copy(row[:, HALF_T:T], raw[t][:, HALF_T:T])
-                nc.scalar.copy(row[:, 0:512], raw[t][:, 0:512])
-                round_on_gpsimd(row[:, 512:HALF_T], raw[t][:, 512:HALF_T])
+            if t == 0:
+                nc.vector.tensor_copy(row[:, ROW_0_ON_SCALAR:T], raw[t][:, ROW_0_ON_SCALAR:T])
+                nc.scalar.copy(row[:, 0:ROW_0_ON_SCALAR], raw[t][:, 0:ROW_0_ON_SCALAR])
             else:
-                for n, engine_copy in enumerate((round_on_gpsimd, nc.vector.tensor_copy, round_on_gpsimd)):
-                    cols = slice(LOADS[t][n], LOADS[t][n + 1])
-                    engine_copy(row[:, cols], raw[t][:, cols])
-            first, end = (0, HALF_S) if t < 2 else (RUN, VECTOR_END)
-            nc.vector.tensor_copy(woven[:, first:end, t], raw[t][:].indirect(entries(first, end)))
-            for first, end in ((HALF_S, S),) if t < 2 else ((0, RUN), (VECTOR_END, S)):
+                round_on_gpsimd(row[:, 0:ROUNDED_EARLY], raw[t][:, 0:ROUNDED_EARLY])
+                cuts = (ROUNDED_EARLY, 1536, T) if t == 3 else (ROUNDED_EARLY, T)
+                for lo, hi in zip(cuts[:-1], cuts[1:]):
+                    nc.vector.tensor_copy(row[:, lo:hi], raw[t][:, lo:hi])
+            share = VECTOR_FIRST_ROWS if t < 2 else VECTOR_LAST_ROWS
+            nc.vector.tensor_copy(woven[:, 0:share, t], raw[t][:].indirect(entries(0, share)))
+            shares = ((share, EARLY), (EARLY, S)) if t == 3 else ((share, S),)
+            for first, end in shares:
                 nc.scalar.activation(woven[:, first:end, t], row[:].indirect(entries(first, end)), ACT.Copy)
 
         codes = keep.tile([P, S], U32, name="codes", align_bytes=64)
@@ -119,41 +115,40 @@ def tile_picked_beamcell_none_l_kernel(
         gates = keep.tile([P, 3, S], F32, name="gates")
         result = keep.tile([P, S], F32, name="result")
         freed = woven[:].rearrange("p n t -> p (n t)").bitcast(F32)
-        picked_at = 2 * 3 * RUN - EARLY
+        picked_at = 3 * RUN
         picked = freed[:, picked_at:picked_at + S]
-        kept = freed[:, picked_at - ON_GPSIMD:picked_at - ON_GPSIMD + S]
+        kept = keep.tile([P, S], F32, name="kept")
 
         def pick(first, end):
             nc.vector.tensor_copy(picked[:, first:end], cell_sb[:].indirect(entries(first, end)))
 
-        for first, end in ((0, RUN), (RUN, HALF_S), (HALF_S, EARLY)):
+        for first, end in ((VECTOR_LAST_ROWS, EARLY), (RUN, VECTOR_LAST_ROWS), (0, RUN)):
             quantise(first, end)
-        pick(0, FIRST_PICK)
+        pick(0, HALF_S)
         for first, end in ((EARLY, 3 * RUN), (3 * RUN, S)):
             quantise(first, end)
-        pick(FIRST_PICK, EARLY)
-        pick(EARLY, S)
+        pick(HALF_S, 3 * RUN)
+        pick(3 * RUN, S)
 
-        for gate, cuts, pieces in (
-            (0, (0, RUN), 1), (0, (RUN, HALF_S, EARLY), 1), (1, (0, HALF_S), 1), (2, (0, HALF_S), 1),
-            (0, (EARLY, 3 * RUN, S), 1), (1, (HALF_S, S), 1), (2, (HALF_S, S), 2),
+        for gate, first, end, bank_tag, pieces in (
+            (0, 0, RUN, "a", 1), (0, RUN, HALF_S, "b", 1), (1, 0, HALF_S, "c", 1),
+            (2, 0, RUN, "d", 1), (2, RUN, HALF_S, "e", 1),
+            (2, HALF_S, S, "f", 1), (0, HALF_S, S, "d", 1), (1, HALF_S, S, "e", 2),
         ):
-            base, total = cuts[0], cuts[-1] - cuts[0]
-            bank = psum.tile([P, total], F32, name="bank_%d_%d" % (gate, base))
-            for first, end in zip(cuts[:-1], cuts[1:]):
-                nc.tensor.matmul_mx(
-                    out=bank[:, first - base:end - base],
-                    lhsT=w_codes[:, gate, :].bitcast(FP8X4),
-                    lhsT_scale=w_planes[:, gate * N:(gate + 1) * N],
-                    rhs=codes[:, first:end].bitcast(FP8X4),
-                    rhs_scale=plane[:, first:end],
-                    start=True,
-                    stop=True,
-                )
-            width = total // pieces
-            for lo in range(0, total, width):
+            bank = psum.tile([P, end - first], F32, name="bank_%d_%d" % (gate, first), tag=bank_tag)
+            nc.tensor.matmul_mx(
+                out=bank[:],
+                lhsT=w_codes[:, gate, :].bitcast(FP8X4),
+                lhsT_scale=w_planes[:, gate * N:(gate + 1) * N],
+                rhs=codes[:, first:end].bitcast(FP8X4),
+                rhs_scale=plane[:, first:end],
+                start=True,
+                stop=True,
+            )
+            width = (end - first) // pieces
+            for lo in range(0, end - first, width):
                 nc.scalar.activation(
-                    gates[:, gate, base + lo:base + lo + width], bank[:, lo:lo + width],
+                    gates[:, gate, first + lo:first + lo + width], bank[:, lo:lo + width],
                     ACT.Tanh if gate == 2 else ACT.Sigmoid,
                 )
 
@@ -161,18 +156,24 @@ def tile_picked_beamcell_none_l_kernel(
             engine.tensor_tensor(kept[:, first:end], gates[:, 0, first:end], picked[:, first:end], ALU.mult)
 
         def fresh_part(first, end):
-            nc.vector.tensor_tensor(gates[:, 0, first:end], gates[:, 1, first:end], gates[:, 2, first:end], ALU.mult)
+            nc.vector.tensor_tensor(result[:, first:end], gates[:, 1, first:end], gates[:, 2, first:end], ALU.mult)
 
-        def finish(first, end):
-            nc.vector.tensor_tensor(result[:, first:end], kept[:, first:end], gates[:, 0, first:end], ALU.add)
+        def add_part(first, end):
+            nc.vector.tensor_tensor(result[:, first:end], kept[:, first:end], result[:, first:end], ALU.add)
+
+        def store(first, end):
             nc.sync.dma_start(out=out[:, first:end], in_=result[:, first:end])
 
-        keep_part(nc.gpsimd, 0, RUN)
-        keep_part(nc.gpsimd, RUN, ON_GPSIMD)
-        fresh_part(0, HALF_S)
+        keep_part(nc.gpsimd, 0, ON_GPSIMD)
+        fresh_part(0, RUN)
+        fresh_part(RUN, HALF_S)
+        add_part(0, RUN)
+        add_part(RUN, ON_GPSIMD)
+        store(0, ON_GPSIMD)
         keep_part(nc.vector, ON_GPSIMD, S)
-        finish(0, HALF_S)
         fresh_part(HALF_S, 3 * RUN)
         fresh_part(3 * RUN, S)
-        finish(HALF_S, 3 * RUN)
-        finish(3 * RUN, S)
+        add_part(ON_GPSIMD, 3 * RUN)
+        store(ON_GPSIMD, 3 * RUN)
+        add_part(3 * RUN, S)
+        store(3 * RUN, S)

@@ -22,11 +22,8 @@ HALF_S = S // 2
 HALF_T = T // 2
 ON_GPSIMD = 448
 EARLY = 640
-VECTOR_LAST_ROWS = 384
-VECTOR_FIRST_ROWS = 448
-ROUNDED_EARLY = 768
-ROW_0_ON_SCALAR = 704
-LOADS = ((0, T), (0, HALF_T, T), (0, HALF_T, T), (0, 768, 1536, T))
+VECTOR_END = 640
+LOADS = ((0, T), (0, HALF_T, T), (0, HALF_T, T), (0, 640, 1536, T))
 
 
 def tile_picked_beamcell_none_l_kernel(
@@ -82,25 +79,24 @@ def tile_picked_beamcell_none_l_kernel(
         def entries(first, end):
             return offsets[:, first // 16:end // 16]
 
-        woven = keep.tile([P, S, 4], BF16, name="woven", tag="woven", align_bytes=64)
+        woven = keep.tile([P, S + 384, 4], BF16, name="woven", tag="woven", align_bytes=64)
 
         def round_on_gpsimd(out, in_):
             nc.gpsimd.tensor_scalar(out, in_, 1.0, 0.0, ALU.mult, ALU.add)
 
+        rounding = (
+            ((round_on_gpsimd, 0, 768), (nc.scalar.copy, 768, T)),
+            ((round_on_gpsimd, 0, 512), (nc.vector.tensor_copy, 512, 1024), (round_on_gpsimd, 1024, T)),
+            ((round_on_gpsimd, 0, 128), (nc.vector.tensor_copy, 128, 1024), (nc.vector.tensor_copy, 1024, T)),
+            ((round_on_gpsimd, 0, 640), (nc.vector.tensor_copy, 640, 1536), (round_on_gpsimd, 1536, T)),
+        )
         for t in range(4):
             row = keep.tile([P, T], BF16, name="row_%d" % t, tag="row_%d" % t, align_bytes=64)
-            if t == 0:
-                nc.vector.tensor_copy(row[:, ROW_0_ON_SCALAR:T], raw[t][:, ROW_0_ON_SCALAR:T])
-                nc.scalar.copy(row[:, 0:ROW_0_ON_SCALAR], raw[t][:, 0:ROW_0_ON_SCALAR])
-            else:
-                round_on_gpsimd(row[:, 0:ROUNDED_EARLY], raw[t][:, 0:ROUNDED_EARLY])
-                cuts = (ROUNDED_EARLY, 1536, T) if t == 3 else (ROUNDED_EARLY, T)
-                for lo, hi in zip(cuts[:-1], cuts[1:]):
-                    nc.vector.tensor_copy(row[:, lo:hi], raw[t][:, lo:hi])
-            share = VECTOR_FIRST_ROWS if t < 2 else VECTOR_LAST_ROWS
-            nc.vector.tensor_copy(woven[:, 0:share, t], raw[t][:].indirect(entries(0, share)))
-            shares = ((share, EARLY), (EARLY, S)) if t == 3 else ((share, S),)
-            for first, end in shares:
+            for engine_copy, lo, hi in rounding[t]:
+                engine_copy(row[:, lo:hi], raw[t][:, lo:hi])
+            first, end = (0, HALF_S) if t < 2 else (RUN, VECTOR_END)
+            nc.vector.tensor_copy(woven[:, first:end, t], raw[t][:].indirect(entries(first, end)))
+            for first, end in ((HALF_S, S),) if t < 2 else ((0, RUN), (VECTOR_END, S)):
                 nc.scalar.activation(woven[:, first:end, t], row[:].indirect(entries(first, end)), ACT.Copy)
 
         codes = keep.tile([P, S], U32, name="codes", align_bytes=64)
@@ -117,12 +113,12 @@ def tile_picked_beamcell_none_l_kernel(
         freed = woven[:].rearrange("p n t -> p (n t)").bitcast(F32)
         picked_at = 3 * RUN
         picked = freed[:, picked_at:picked_at + S]
-        kept = keep.tile([P, S], F32, name="kept")
+        kept = freed[:, picked_at + S:picked_at + 2 * S]
 
         def pick(first, end):
             nc.vector.tensor_copy(picked[:, first:end], cell_sb[:].indirect(entries(first, end)))
 
-        for first, end in ((VECTOR_LAST_ROWS, EARLY), (RUN, VECTOR_LAST_ROWS), (0, RUN)):
+        for first, end in ((RUN, HALF_S), (HALF_S, EARLY), (0, RUN)):
             quantise(first, end)
         pick(0, HALF_S)
         for first, end in ((EARLY, 3 * RUN), (3 * RUN, S)):
@@ -131,8 +127,9 @@ def tile_picked_beamcell_none_l_kernel(
         pick(3 * RUN, S)
 
         for gate, first, end, bank_tag, pieces in (
-            (0, 0, RUN, "a", 1), (0, RUN, HALF_S, "b", 1), (1, 0, HALF_S, "c", 1),
-            (2, 0, RUN, "d", 1), (2, RUN, HALF_S, "e", 1),
+            (0, 0, RUN, "a", 1), (0, RUN, HALF_S, "b", 1),
+            (1, 0, RUN, "c", 1), (2, 0, RUN, "d", 1), (1, RUN, HALF_S, "g", 1), (2, RUN, HALF_S, "e", 1),
+
             (2, HALF_S, S, "f", 1), (0, HALF_S, S, "d", 1), (1, HALF_S, S, "e", 2),
         ):
             bank = psum.tile([P, end - first], F32, name="bank_%d_%d" % (gate, first), tag=bank_tag)

@@ -20,7 +20,6 @@ RUN = 256
 RUNS = S // RUN
 HALF_S = S // 2
 HALF_T = T // 2
-ON_GPSIMD = 448
 EARLY = 640
 VECTOR_END = 640
 LOADS = ((0, T), (0, HALF_T, T), (0, HALF_T, T), (0, 640, 1536, T))
@@ -79,7 +78,7 @@ def tile_picked_beamcell_none_l_kernel(
         def entries(first, end):
             return offsets[:, first // 16:end // 16]
 
-        woven = keep.tile([P, S + 384, 4], BF16, name="woven", tag="woven", align_bytes=64)
+        woven = keep.tile([P, S, 4], BF16, name="woven", tag="woven", align_bytes=64)
 
         def round_on_gpsimd(out, in_):
             nc.gpsimd.tensor_scalar(out, in_, 1.0, 0.0, ALU.mult, ALU.add)
@@ -110,21 +109,17 @@ def tile_picked_beamcell_none_l_kernel(
 
         gates = keep.tile([P, 3, S], F32, name="gates")
         result = keep.tile([P, S], F32, name="result")
-        freed = woven[:].rearrange("p n t -> p (n t)").bitcast(F32)
-        picked_at = 3 * RUN
-        picked = freed[:, picked_at:picked_at + S]
-        kept = freed[:, picked_at + S:picked_at + 2 * S]
+        picked = keep.tile([P, S], F32, name="picked")
+        kept = keep.tile([P, S], F32, name="kept")
 
         def pick(first, end):
             nc.vector.tensor_copy(picked[:, first:end], cell_sb[:].indirect(entries(first, end)))
 
         for first, end in ((RUN, HALF_S), (HALF_S, EARLY), (0, RUN)):
             quantise(first, end)
-        pick(0, HALF_S)
+        pick(HALF_S, S)
         for first, end in ((EARLY, 3 * RUN), (3 * RUN, S)):
             quantise(first, end)
-        pick(HALF_S, 3 * RUN)
-        pick(3 * RUN, S)
 
         for gate, first, end, bank_tag, pieces in (
             (0, 0, RUN, "a", 1), (0, RUN, HALF_S, "b", 1),
@@ -161,16 +156,18 @@ def tile_picked_beamcell_none_l_kernel(
         def store(first, end):
             nc.sync.dma_start(out=out[:, first:end], in_=result[:, first:end])
 
-        keep_part(nc.gpsimd, 0, ON_GPSIMD)
+        nc.vector.tensor_tensor(
+            kept[:, 0:HALF_S], cell_sb[:].indirect(entries(0, HALF_S)), gates[:, 0, 0:HALF_S], ALU.mult
+        )
         fresh_part(0, RUN)
         fresh_part(RUN, HALF_S)
         add_part(0, RUN)
-        add_part(RUN, ON_GPSIMD)
-        store(0, ON_GPSIMD)
-        keep_part(nc.vector, ON_GPSIMD, S)
+        add_part(RUN, HALF_S)
+        store(0, HALF_S)
+        keep_part(nc.vector, HALF_S, S)
         fresh_part(HALF_S, 3 * RUN)
         fresh_part(3 * RUN, S)
-        add_part(ON_GPSIMD, 3 * RUN)
-        store(ON_GPSIMD, 3 * RUN)
+        add_part(HALF_S, 3 * RUN)
+        store(HALF_S, 3 * RUN)
         add_part(3 * RUN, S)
         store(3 * RUN, S)

@@ -17,12 +17,10 @@ ALU = mybir.AluOpType
 
 P = 128
 RUN = 256
-RUNS = S // RUN
 HALF_S = S // 2
 HALF_T = T // 2
-EARLY = 640
-VECTOR_END = 640
-LOADS = ((0, T), (0, HALF_T, T), (0, HALF_T, T), (0, 640, 1536, T))
+MIDDLE_SHARE = 448
+LOADS = {2: (0, T), 0: (0, HALF_T, T), 1: (0, HALF_T, T), 3: (0, 768, 1664, T)}
 
 
 def tile_picked_beamcell_none_l_kernel(
@@ -42,23 +40,13 @@ def tile_picked_beamcell_none_l_kernel(
 
         offsets = keep.tile([P, S // 16], U16, name="offsets")
         x_rows = xT.rearrange("(p t) c -> p t c", t=4)
+        raw = {}
 
         def load_row(t):
-            tile = keep.tile([P, T], F32, name="raw_%d" % t)
+            raw[t] = keep.tile([P, T], F32, name="raw_%d" % t)
             for first, end in zip(LOADS[t][:-1], LOADS[t][1:]):
-                nc.sync.dma_start(out=tile[:, first:end], in_=x_rows[:, t, first:end])
-            return tile
+                nc.sync.dma_start(out=raw[t][:, first:end], in_=x_rows[:, t, first:end])
 
-        raw = [load_row(0)]
-        nc.sync.dma_start(offsets[:], offs)
-        for t in (1, 2, 3):
-            raw.append(load_row(t))
-        plane = keep.tile([P, S], U8, name="plane", align_bytes=64)
-        staged = plane[:, EARLY:S]
-        for gate, scales in enumerate((w1_scales, w2_scales, w3_scales)):
-            nc.sync.dma_start(out=staged[0:16, gate * N:(gate + 1) * N].bitcast(I32), in_=scales[0].bitcast(I32))
-        cell_sb = keep.tile([P, T], F32, name="cell_sb")
-        nc.sync.dma_start(out=cell_sb[:], in_=cell)
         w_codes = keep.tile([P, 3, N], U32, name="w_codes", align_bytes=64)
 
         def load_codes(gate, words):
@@ -66,66 +54,67 @@ def tile_picked_beamcell_none_l_kernel(
                 out=w_codes[:, gate, :].bitcast(I32), in_=words[0].rearrange("p n t -> p (n t)").bitcast(I32)
             )
 
+        load_row(2)
+        nc.sync.dma_start(offsets[:], offs)
+        load_row(0)
+        load_row(1)
+        for gate, scales in enumerate((w1_scales, w2_scales, w3_scales)):
+            nc.sync.dma_start(out=w_planes[0:16, gate * N:(gate + 1) * N].bitcast(I32), in_=scales[0].bitcast(I32))
+        load_row(3)
         load_codes(0, w1_words)
-        for quadrant in range(4):
+        for quadrant in range(1, 4):
             nc.sync.dma_start(
                 out=w_planes[32 * quadrant:32 * quadrant + 4, :].bitcast(I32),
-                in_=staged[4 * quadrant:4 * quadrant + 4, :].bitcast(I32),
+                in_=w_planes[4 * quadrant:4 * quadrant + 4, :].bitcast(I32),
             )
+        cell_sb = keep.tile([P, T], F32, name="cell_sb")
+        nc.sync.dma_start(out=cell_sb[:], in_=cell)
         load_codes(1, w2_words)
         load_codes(2, w3_words)
 
         def entries(first, end):
             return offsets[:, first // 16:end // 16]
 
-        woven = keep.tile([P, S, 4], BF16, name="woven", tag="woven", align_bytes=64)
+        woven = keep.tile([P, S, 4], BF16, name="woven", align_bytes=64)
 
         def round_on_gpsimd(out, in_):
             nc.gpsimd.tensor_scalar(out, in_, 1.0, 0.0, ALU.mult, ALU.add)
 
-        rounding = (
-            ((round_on_gpsimd, 0, 768), (nc.scalar.copy, 768, T)),
-            ((round_on_gpsimd, 0, 512), (nc.vector.tensor_copy, 512, 1024), (round_on_gpsimd, 1024, T)),
-            ((round_on_gpsimd, 0, 128), (nc.vector.tensor_copy, 128, 1024), (nc.vector.tensor_copy, 1024, T)),
-            ((round_on_gpsimd, 0, 640), (nc.vector.tensor_copy, 640, 1536), (round_on_gpsimd, 1536, T)),
-        )
-        for t in range(4):
-            row = keep.tile([P, T], BF16, name="row_%d" % t, tag="row_%d" % t, align_bytes=64)
+        middle = ((round_on_gpsimd, 0, 512), (nc.vector.tensor_copy, 512, HALF_T), (nc.vector.tensor_copy, HALF_T, T))
+        rounding = {
+            2: ((round_on_gpsimd, 0, 896), (nc.scalar.copy, 896, T)),
+            0: middle,
+            1: middle,
+            3: ((round_on_gpsimd, 0, 768), (nc.vector.tensor_copy, 768, 1664), (round_on_gpsimd, 1664, T)),
+        }
+        on_vector = {2: (0, HALF_S), 0: (0, MIDDLE_SHARE), 1: (0, MIDDLE_SHARE), 3: (0, RUN, HALF_S)}
+        on_scalar = {2: (HALF_S, S), 0: (MIDDLE_SHARE, S), 1: (MIDDLE_SHARE, S), 3: (HALF_S, 3 * RUN, S)}
+        for t in (2, 0, 1, 3):
+            row = keep.tile([P, T], BF16, name="row_%d" % t, align_bytes=64)
             for engine_copy, lo, hi in rounding[t]:
                 engine_copy(row[:, lo:hi], raw[t][:, lo:hi])
-            first, end = (0, HALF_S) if t < 2 else (RUN, VECTOR_END)
-            nc.vector.tensor_copy(woven[:, first:end, t], raw[t][:].indirect(entries(first, end)))
-            for first, end in ((HALF_S, S),) if t < 2 else ((0, RUN), (VECTOR_END, S)):
+            for first, end in zip(on_vector[t][:-1], on_vector[t][1:]):
+                nc.vector.tensor_copy(woven[:, first:end, t], raw[t][:].indirect(entries(first, end)))
+            for first, end in zip(on_scalar[t][:-1], on_scalar[t][1:]):
                 nc.scalar.activation(woven[:, first:end, t], row[:].indirect(entries(first, end)), ACT.Copy)
 
         codes = keep.tile([P, S], U32, name="codes", align_bytes=64)
-
-        def quantise(first, end):
+        plane = keep.tile([P, S], U8, name="plane", align_bytes=64)
+        for first in range(0, S, RUN):
             nc.vector.quantize_mx(
-                out=codes[:, first:end].bitcast(FP8X4),
-                scales=plane[:, first:end],
-                in_=woven[:, first:end, :].rearrange("p n t -> p (n t)"),
+                out=codes[:, first:first + RUN].bitcast(FP8X4),
+                scales=plane[:, first:first + RUN],
+                in_=woven[:, first:first + RUN, :].rearrange("p n t -> p (n t)"),
             )
 
         gates = keep.tile([P, 3, S], F32, name="gates")
-        result = keep.tile([P, S], F32, name="result")
-        picked = keep.tile([P, S], F32, name="picked")
         kept = keep.tile([P, S], F32, name="kept")
-
-        def pick(first, end):
-            nc.vector.tensor_copy(picked[:, first:end], cell_sb[:].indirect(entries(first, end)))
-
-        for first, end in ((RUN, HALF_S), (HALF_S, EARLY), (0, RUN)):
-            quantise(first, end)
-        pick(HALF_S, S)
-        for first, end in ((EARLY, 3 * RUN), (3 * RUN, S)):
-            quantise(first, end)
+        result = keep.tile([P, S], F32, name="result")
 
         for gate, first, end, bank_tag, pieces in (
-            (0, 0, RUN, "a", 1), (0, RUN, HALF_S, "b", 1),
-            (1, 0, RUN, "c", 1), (2, 0, RUN, "d", 1), (1, RUN, HALF_S, "g", 1), (2, RUN, HALF_S, "e", 1),
-
-            (2, HALF_S, S, "f", 1), (0, HALF_S, S, "d", 1), (1, HALF_S, S, "e", 2),
+            (0, 0, RUN, "a", 1), (0, RUN, HALF_S, "b", 1), (0, HALF_S, 3 * RUN, "c", 1), (0, 3 * RUN, S, "d", 1),
+            (1, 0, RUN, "a", 1), (2, 0, RUN, "e", 1), (1, RUN, HALF_S, "f", 1), (2, RUN, HALF_S, "g", 1),
+            (2, HALF_S, S, "h", 1), (1, HALF_S, S, "f", 2),
         ):
             bank = psum.tile([P, end - first], F32, name="bank_%d_%d" % (gate, first), tag=bank_tag)
             nc.tensor.matmul_mx(
@@ -144,8 +133,10 @@ def tile_picked_beamcell_none_l_kernel(
                     ACT.Tanh if gate == 2 else ACT.Sigmoid,
                 )
 
-        def keep_part(engine, first, end):
-            engine.tensor_tensor(kept[:, first:end], gates[:, 0, first:end], picked[:, first:end], ALU.mult)
+        def keep_part(first, end):
+            nc.vector.tensor_tensor(
+                kept[:, first:end], cell_sb[:].indirect(entries(first, end)), gates[:, 0, first:end], ALU.mult
+            )
 
         def fresh_part(first, end):
             nc.vector.tensor_tensor(result[:, first:end], gates[:, 1, first:end], gates[:, 2, first:end], ALU.mult)
@@ -156,15 +147,14 @@ def tile_picked_beamcell_none_l_kernel(
         def store(first, end):
             nc.sync.dma_start(out=out[:, first:end], in_=result[:, first:end])
 
-        nc.vector.tensor_tensor(
-            kept[:, 0:HALF_S], cell_sb[:].indirect(entries(0, HALF_S)), gates[:, 0, 0:HALF_S], ALU.mult
-        )
+        keep_part(0, RUN)
+        keep_part(RUN, HALF_S)
+        keep_part(HALF_S, S)
         fresh_part(0, RUN)
         fresh_part(RUN, HALF_S)
         add_part(0, RUN)
         add_part(RUN, HALF_S)
         store(0, HALF_S)
-        keep_part(nc.vector, HALF_S, S)
         fresh_part(HALF_S, 3 * RUN)
         fresh_part(3 * RUN, S)
         add_part(HALF_S, 3 * RUN)

@@ -19,8 +19,13 @@ P = 128
 RUN = 256
 HALF_S = S // 2
 HALF_T = T // 2
-MIDDLE_SHARE = 448
-LOADS = {2: (0, T), 0: (0, HALF_T, T), 1: (0, HALF_T, T), 3: (0, 768, 1664, T)}
+F_GATE, Q_GATE, G_GATE = 0, 1, 2
+
+ROW_ORDER = (2, 0, 1, 3)
+MIDDLE_SHARE = 384
+ON_GPSIMD = 896
+LAST_CUTS = (0, 768, 1664, T)
+LOAD_CUTS = {2: (0, T), 0: (0, HALF_T, T), 1: (0, HALF_T, T), 3: LAST_CUTS}
 
 
 def tile_picked_beamcell_none_l_kernel(
@@ -31,23 +36,30 @@ def tile_picked_beamcell_none_l_kernel(
         keep = ctx.enter_context(tc.tile_pool(name="keep", bufs=1))
         psum = ctx.enter_context(tc.psum_pool(name="psum", bufs=1))
 
-        w_planes = keep.tile([P, 3 * N], U8, name="w_planes", align_bytes=64)
-        nc.vector.memset(w_planes[:].bitcast(I32), 0)
+        w_scales = keep.tile([P, 3 * N], U8, name="w_scales", align_bytes=64)
+        nc.vector.memset(w_scales[:].bitcast(I32), 0)
 
         warm = keep.tile([P, 2], F32, name="warm")
         nc.vector.memset(warm[:, 0:1], 0.0)
         nc.scalar.activation(warm[:, 1:2], warm[:, 0:1], ACT.Sigmoid)
 
+        own_words = LAST_CUTS[2] // 2
+        shared = keep.tile([P, own_words + T], F32, name="shared", align_bytes=64)
+        raw = {1: shared[:, own_words:]}
+        rounded = {3: shared[:].bitcast(BF16)[:, 0:T]}
+        for t in (2, 0, 3):
+            raw[t] = keep.tile([P, T], F32, name="raw_%d" % t)[:]
+        for t in (2, 0, 1):
+            rounded[t] = keep.tile([P, T], BF16, name="rounded_%d" % t, align_bytes=64)[:]
+
         offsets = keep.tile([P, S // 16], U16, name="offsets")
+        w_codes = keep.tile([P, 3, N], U32, name="w_codes", align_bytes=64)
+        cell_sb = keep.tile([P, T], F32, name="cell_sb")
         x_rows = xT.rearrange("(p t) c -> p t c", t=4)
-        raw = {}
 
         def load_row(t):
-            raw[t] = keep.tile([P, T], F32, name="raw_%d" % t)
-            for first, end in zip(LOADS[t][:-1], LOADS[t][1:]):
+            for first, end in zip(LOAD_CUTS[t][:-1], LOAD_CUTS[t][1:]):
                 nc.sync.dma_start(out=raw[t][:, first:end], in_=x_rows[:, t, first:end])
-
-        w_codes = keep.tile([P, 3, N], U32, name="w_codes", align_bytes=64)
 
         def load_codes(gate, words):
             nc.sync.dma_start(
@@ -59,105 +71,107 @@ def tile_picked_beamcell_none_l_kernel(
         load_row(0)
         load_row(1)
         for gate, scales in enumerate((w1_scales, w2_scales, w3_scales)):
-            nc.sync.dma_start(out=w_planes[0:16, gate * N:(gate + 1) * N].bitcast(I32), in_=scales[0].bitcast(I32))
+            nc.sync.dma_start(out=w_scales[0:16, gate * N:(gate + 1) * N].bitcast(I32), in_=scales[0].bitcast(I32))
         load_row(3)
-        load_codes(0, w1_words)
+        load_codes(F_GATE, w1_words)
         for quadrant in range(1, 4):
             nc.sync.dma_start(
-                out=w_planes[32 * quadrant:32 * quadrant + 4, :].bitcast(I32),
-                in_=w_planes[4 * quadrant:4 * quadrant + 4, :].bitcast(I32),
+                out=w_scales[32 * quadrant:32 * quadrant + 4, :].bitcast(I32),
+                in_=w_scales[4 * quadrant:4 * quadrant + 4, :].bitcast(I32),
             )
-        cell_sb = keep.tile([P, T], F32, name="cell_sb")
         nc.sync.dma_start(out=cell_sb[:], in_=cell)
-        load_codes(1, w2_words)
-        load_codes(2, w3_words)
+        load_codes(Q_GATE, w2_words)
+        load_codes(G_GATE, w3_words)
 
         def entries(first, end):
             return offsets[:, first // 16:end // 16]
 
-        woven = keep.tile([P, S, 4], BF16, name="woven", align_bytes=64)
+        def round_on_gpsimd(out_cols, in_cols):
+            nc.gpsimd.tensor_scalar(out_cols, in_cols, 1.0, 0.0, ALU.mult, ALU.add)
 
-        def round_on_gpsimd(out, in_):
-            nc.gpsimd.tensor_scalar(out, in_, 1.0, 0.0, ALU.mult, ALU.add)
-
-        middle = ((round_on_gpsimd, 0, 512), (nc.vector.tensor_copy, 512, HALF_T), (nc.vector.tensor_copy, HALF_T, T))
+        middle = ((round_on_gpsimd, 0, ON_GPSIMD), (nc.vector.tensor_copy, ON_GPSIMD, T))
         rounding = {
-            2: ((round_on_gpsimd, 0, 896), (nc.scalar.copy, 896, T)),
+            2: ((round_on_gpsimd, 0, ON_GPSIMD), (nc.scalar.copy, ON_GPSIMD, T)),
             0: middle,
             1: middle,
-            3: ((round_on_gpsimd, 0, 768), (nc.vector.tensor_copy, 768, 1664), (round_on_gpsimd, 1664, T)),
+            3: zip((round_on_gpsimd, nc.vector.tensor_copy, round_on_gpsimd), LAST_CUTS[:-1], LAST_CUTS[1:]),
         }
         on_vector = {2: (0, HALF_S), 0: (0, MIDDLE_SHARE), 1: (0, MIDDLE_SHARE), 3: (0, RUN, HALF_S)}
         on_scalar = {2: (HALF_S, S), 0: (MIDDLE_SHARE, S), 1: (MIDDLE_SHARE, S), 3: (HALF_S, 3 * RUN, S)}
-        for t in (2, 0, 1, 3):
-            row = keep.tile([P, T], BF16, name="row_%d" % t, align_bytes=64)
-            for engine_copy, lo, hi in rounding[t]:
-                engine_copy(row[:, lo:hi], raw[t][:, lo:hi])
-            for first, end in zip(on_vector[t][:-1], on_vector[t][1:]):
-                nc.vector.tensor_copy(woven[:, first:end, t], raw[t][:].indirect(entries(first, end)))
-            for first, end in zip(on_scalar[t][:-1], on_scalar[t][1:]):
-                nc.scalar.activation(woven[:, first:end, t], row[:].indirect(entries(first, end)), ACT.Copy)
 
-        codes = keep.tile([P, S], U32, name="codes", align_bytes=64)
-        plane = keep.tile([P, S], U8, name="plane", align_bytes=64)
+        woven = keep.tile([P, S, 4], BF16, name="woven", align_bytes=64)
+        for t in ROW_ORDER:
+            for round_columns, first, end in rounding[t]:
+                round_columns(rounded[t][:, first:end], raw[t][:, first:end])
+            for first, end in zip(on_vector[t][:-1], on_vector[t][1:]):
+                nc.vector.tensor_copy(woven[:, first:end, t], raw[t].indirect(entries(first, end)))
+            for first, end in zip(on_scalar[t][:-1], on_scalar[t][1:]):
+                nc.scalar.activation(woven[:, first:end, t], rounded[t].indirect(entries(first, end)), ACT.Copy)
+
+        x_codes = keep.tile([P, S], U32, name="x_codes", align_bytes=64)
+        x_scales = keep.tile([P, S], U8, name="x_scales", align_bytes=64)
         for first in range(0, S, RUN):
             nc.vector.quantize_mx(
-                out=codes[:, first:first + RUN].bitcast(FP8X4),
-                scales=plane[:, first:first + RUN],
+                out=x_codes[:, first:first + RUN].bitcast(FP8X4),
+                scales=x_scales[:, first:first + RUN],
                 in_=woven[:, first:first + RUN, :].rearrange("p n t -> p (n t)"),
             )
 
         gates = keep.tile([P, 3, S], F32, name="gates")
-        kept = keep.tile([P, S], F32, name="kept")
-        result = keep.tile([P, S], F32, name="result")
 
-        for gate, first, end, bank_tag, pieces in (
-            (0, 0, RUN, "a", 1), (0, RUN, HALF_S, "b", 1), (0, HALF_S, 3 * RUN, "c", 1), (0, 3 * RUN, S, "d", 1),
-            (1, 0, RUN, "a", 1), (2, 0, RUN, "e", 1), (1, RUN, HALF_S, "f", 1), (2, RUN, HALF_S, "g", 1),
-            (2, HALF_S, S, "h", 1), (1, HALF_S, S, "f", 2),
-        ):
+        def make_gate(gate, first, end, bank_tag, width):
             bank = psum.tile([P, end - first], F32, name="bank_%d_%d" % (gate, first), tag=bank_tag)
             nc.tensor.matmul_mx(
                 out=bank[:],
                 lhsT=w_codes[:, gate, :].bitcast(FP8X4),
-                lhsT_scale=w_planes[:, gate * N:(gate + 1) * N],
-                rhs=codes[:, first:end].bitcast(FP8X4),
-                rhs_scale=plane[:, first:end],
+                lhsT_scale=w_scales[:, gate * N:(gate + 1) * N],
+                rhs=x_codes[:, first:end].bitcast(FP8X4),
+                rhs_scale=x_scales[:, first:end],
                 start=True,
                 stop=True,
             )
-            width = (end - first) // pieces
-            for lo in range(0, end - first, width):
+            for lo in range(first, end, width):
                 nc.scalar.activation(
-                    gates[:, gate, first + lo:first + lo + width], bank[:, lo:lo + width],
-                    ACT.Tanh if gate == 2 else ACT.Sigmoid,
+                    gates[:, gate, lo:lo + width], bank[:, lo - first:lo - first + width],
+                    ACT.Tanh if gate == G_GATE else ACT.Sigmoid,
                 )
 
-        def keep_part(first, end):
+        for run in range(4):
+            make_gate(F_GATE, run * RUN, (run + 1) * RUN, "f%d" % run, RUN)
+        make_gate(Q_GATE, 0, RUN, "f0", RUN)
+        make_gate(G_GATE, 0, RUN, "g0", RUN)
+        make_gate(Q_GATE, RUN, HALF_S, "q1", RUN)
+        make_gate(G_GATE, RUN, HALF_S, "g1", RUN)
+        make_gate(G_GATE, HALF_S, S, "g2", HALF_S)
+        make_gate(Q_GATE, HALF_S, S, "q1", RUN)
+
+        kept = keep.tile([P, S], F32, name="kept")
+        result = keep.tile([P, S], F32, name="result")
+
+        for first, end in ((0, RUN), (RUN, HALF_S), (HALF_S, S)):
             nc.vector.tensor_tensor(
-                kept[:, first:end], cell_sb[:].indirect(entries(first, end)), gates[:, 0, first:end], ALU.mult
+                kept[:, first:end], cell_sb[:].indirect(entries(first, end)), gates[:, F_GATE, first:end], ALU.mult
             )
 
-        def fresh_part(first, end):
-            nc.vector.tensor_tensor(result[:, first:end], gates[:, 1, first:end], gates[:, 2, first:end], ALU.mult)
+        def multiply_q_g(run):
+            cols = slice(run * RUN, (run + 1) * RUN)
+            nc.vector.tensor_tensor(result[:, cols], gates[:, Q_GATE, cols], gates[:, G_GATE, cols], ALU.mult)
 
-        def add_part(first, end):
-            nc.vector.tensor_tensor(result[:, first:end], kept[:, first:end], result[:, first:end], ALU.add)
+        def add_kept(run):
+            cols = slice(run * RUN, (run + 1) * RUN)
+            nc.vector.tensor_tensor(result[:, cols], kept[:, cols], result[:, cols], ALU.add)
 
         def store(first, end):
             nc.sync.dma_start(out=out[:, first:end], in_=result[:, first:end])
 
-        keep_part(0, RUN)
-        keep_part(RUN, HALF_S)
-        keep_part(HALF_S, S)
-        fresh_part(0, RUN)
-        fresh_part(RUN, HALF_S)
-        add_part(0, RUN)
-        add_part(RUN, HALF_S)
+        multiply_q_g(0)
+        multiply_q_g(1)
+        add_kept(0)
+        add_kept(1)
         store(0, HALF_S)
-        fresh_part(HALF_S, 3 * RUN)
-        fresh_part(3 * RUN, S)
-        add_part(HALF_S, 3 * RUN)
+        multiply_q_g(2)
+        multiply_q_g(3)
+        add_kept(2)
         store(HALF_S, 3 * RUN)
-        add_part(3 * RUN, S)
+        add_kept(3)
         store(3 * RUN, S)

@@ -17,15 +17,10 @@ ALU = mybir.AluOpType
 
 P = 128
 RUN = 256
-HALF_S = S // 2
-HALF_T = T // 2
 F_GATE, Q_GATE, G_GATE = 0, 1, 2
-
-ROW_ORDER = (2, 0, 1, 3)
-MIDDLE_SHARE = 384
-ON_GPSIMD = 896
-LAST_CUTS = (0, 768, 1664, T)
-LOAD_CUTS = {2: (0, T), 0: (0, HALF_T, T), 1: (0, HALF_T, T), 3: LAST_CUTS}
+OWN = 256
+HALF = 512
+LAST_CUTS = (256, 384, 512, 768, 1024)
 
 
 def tile_picked_beamcell_none_l_kernel(
@@ -43,84 +38,82 @@ def tile_picked_beamcell_none_l_kernel(
         nc.vector.memset(warm[:, 0:1], 0.0)
         nc.scalar.activation(warm[:, 1:2], warm[:, 0:1], ACT.Sigmoid)
 
-        own_words = LAST_CUTS[2] // 2
-        shared = keep.tile([P, own_words + T], F32, name="shared", align_bytes=64)
-        raw = {1: shared[:, own_words:]}
-        rounded = {3: shared[:].bitcast(BF16)[:, 0:T]}
-        for t in (2, 0, 3):
-            raw[t] = keep.tile([P, T], F32, name="raw_%d" % t)[:]
-        for t in (2, 0, 1):
-            rounded[t] = keep.tile([P, T], BF16, name="rounded_%d" % t, align_bytes=64)[:]
-
+        raw = [keep.tile([P, T], F32, name="raw_%d" % t) for t in range(4)]
         offsets = keep.tile([P, S // 16], U16, name="offsets")
         w_codes = keep.tile([P, 3, N], U32, name="w_codes", align_bytes=64)
         cell_sb = keep.tile([P, T], F32, name="cell_sb")
         x_rows = xT.rearrange("(p t) c -> p t c", t=4)
 
-        def load_row(t):
-            for first, end in zip(LOAD_CUTS[t][:-1], LOAD_CUTS[t][1:]):
-                nc.sync.dma_start(out=raw[t][:, first:end], in_=x_rows[:, t, first:end])
-
-        def load_codes(gate, words):
-            nc.sync.dma_start(
-                out=w_codes[:, gate, :].bitcast(I32), in_=words[0].rearrange("p n t -> p (n t)").bitcast(I32)
-            )
-
-        load_row(2)
+        nc.sync.dma_start(out=raw[0][:], in_=x_rows[:, 0, :])
         nc.sync.dma_start(offsets[:], offs)
-        load_row(0)
-        load_row(1)
         for gate, scales in enumerate((w1_scales, w2_scales, w3_scales)):
             nc.sync.dma_start(out=w_scales[0:16, gate * N:(gate + 1) * N].bitcast(I32), in_=scales[0].bitcast(I32))
-        load_row(3)
-        load_codes(F_GATE, w1_words)
+        nc.sync.dma_start(out=raw[1][:], in_=x_rows[:, 1, :])
+        nc.sync.dma_start(out=raw[2][:], in_=x_rows[:, 2, :])
         for quadrant in range(1, 4):
             nc.sync.dma_start(
                 out=w_scales[32 * quadrant:32 * quadrant + 4, :].bitcast(I32),
                 in_=w_scales[4 * quadrant:4 * quadrant + 4, :].bitcast(I32),
             )
+        nc.sync.dma_start(out=raw[3][:], in_=x_rows[:, 3, :])
+        for gate, words in enumerate((w1_words, w2_words, w3_words)):
+            nc.sync.dma_start(
+                out=w_codes[:, gate, :].bitcast(I32), in_=words[0].rearrange("p n t -> p (n t)").bitcast(I32)
+            )
         nc.sync.dma_start(out=cell_sb[:], in_=cell)
-        load_codes(Q_GATE, w2_words)
-        load_codes(G_GATE, w3_words)
 
         def entries(first, end):
             return offsets[:, first // 16:end // 16]
 
-        def round_on_gpsimd(out_cols, in_cols):
-            nc.gpsimd.tensor_scalar(out_cols, in_cols, 1.0, 0.0, ALU.mult, ALU.add)
-
-        middle = ((round_on_gpsimd, 0, ON_GPSIMD), (nc.vector.tensor_copy, ON_GPSIMD, T))
-        rounding = {
-            2: ((round_on_gpsimd, 0, ON_GPSIMD), (nc.scalar.copy, ON_GPSIMD, T)),
-            0: middle,
-            1: middle,
-            3: zip((round_on_gpsimd, nc.vector.tensor_copy, round_on_gpsimd), LAST_CUTS[:-1], LAST_CUTS[1:]),
-        }
-        on_vector = {2: (0, HALF_S), 0: (0, MIDDLE_SHARE), 1: (0, MIDDLE_SHARE), 3: (0, RUN, HALF_S)}
-        on_scalar = {2: (HALF_S, S), 0: (MIDDLE_SHARE, S), 1: (MIDDLE_SHARE, S), 3: (HALF_S, 3 * RUN, S)}
-
         woven = keep.tile([P, S, 4], BF16, name="woven", align_bytes=64)
-        for t in ROW_ORDER:
-            for round_columns, first, end in rounding[t]:
-                round_columns(rounded[t][:, first:end], raw[t][:, first:end])
-            for first, end in zip(on_vector[t][:-1], on_vector[t][1:]):
-                nc.vector.tensor_copy(woven[:, first:end, t], raw[t].indirect(entries(first, end)))
-            for first, end in zip(on_scalar[t][:-1], on_scalar[t][1:]):
-                nc.scalar.activation(woven[:, first:end, t], rounded[t].indirect(entries(first, end)), ACT.Copy)
-
+        planes = [keep.tile([P, 2, S - OWN], BF16, name="planes_%d" % h, align_bytes=64) for h in range(2)]
         x_codes = keep.tile([P, S], U32, name="x_codes", align_bytes=64)
         x_scales = keep.tile([P, S], U8, name="x_scales", align_bytes=64)
-        for first in range(0, S, RUN):
-            nc.vector.quantize_mx(
-                out=x_codes[:, first:first + RUN].bitcast(FP8X4),
-                scales=x_scales[:, first:first + RUN],
-                in_=woven[:, first:first + RUN, :].rearrange("p n t -> p (n t)"),
+
+        def gather_own(t):
+            nc.vector.tensor_copy(woven[:, 0:OWN, t], raw[t][:].indirect(entries(0, OWN)))
+
+        def gather_plane(t, first, end):
+            nc.scalar.activation(
+                planes[t // 2][:, t % 2, first - OWN:end - OWN], raw[t][:].indirect(entries(first, end)), ACT.Copy
             )
 
-        gates = keep.tile([P, 3, S], F32, name="gates")
+        def place(pair, first, end):
+            nc.vector.tensor_copy(
+                woven[:, first:end, 2 * pair:2 * pair + 2],
+                planes[pair][:, :, first - OWN:end - OWN].rearrange("p t n -> p n t"),
+            )
 
-        def make_gate(gate, first, end, bank_tag, width):
-            bank = psum.tile([P, end - first], F32, name="bank_%d_%d" % (gate, first), tag=bank_tag)
+        def quantise(run):
+            cols = slice(run * RUN, (run + 1) * RUN)
+            nc.vector.quantize_mx(
+                out=x_codes[:, cols].bitcast(FP8X4),
+                scales=x_scales[:, cols],
+                in_=woven[:, cols, :].rearrange("p n t -> p (n t)"),
+            )
+
+        for t in range(3):
+            gather_own(t)
+            gather_plane(t, OWN, S)
+            if t == 1:
+                place(0, OWN, S)
+        gather_own(3)
+        for first, end in zip(LAST_CUTS[:-1], LAST_CUTS[1:]):
+            gather_plane(3, first, end)
+        place(1, LAST_CUTS[0], LAST_CUTS[1])
+        quantise(0)
+        place(1, LAST_CUTS[1], LAST_CUTS[2])
+        place(1, LAST_CUTS[2], LAST_CUTS[3])
+        quantise(1)
+        place(1, LAST_CUTS[3], LAST_CUTS[4])
+        quantise(2)
+        quantise(3)
+
+        gates = keep.tile([P, 3, HALF], F32, name="gates")
+        f_late = keep.tile([P, HALF], F32, name="f_late")
+
+        def make_gate(gate, first, end, tag, width, dest):
+            bank = psum.tile([P, end - first], F32, name="bank_%d_%d" % (gate, first), tag=tag)
             nc.tensor.matmul_mx(
                 out=bank[:],
                 lhsT=w_codes[:, gate, :].bitcast(FP8X4),
@@ -130,48 +123,46 @@ def tile_picked_beamcell_none_l_kernel(
                 start=True,
                 stop=True,
             )
-            for lo in range(first, end, width):
+            for lo in range(0, end - first, width):
                 nc.scalar.activation(
-                    gates[:, gate, lo:lo + width], bank[:, lo - first:lo - first + width],
-                    ACT.Tanh if gate == G_GATE else ACT.Sigmoid,
+                    dest[:, lo:lo + width], bank[:, lo:lo + width], ACT.Tanh if gate == G_GATE else ACT.Sigmoid
                 )
 
-        for run in range(4):
-            make_gate(F_GATE, run * RUN, (run + 1) * RUN, "f%d" % run, RUN)
-        make_gate(Q_GATE, 0, RUN, "f0", RUN)
-        make_gate(G_GATE, 0, RUN, "g0", RUN)
-        make_gate(Q_GATE, RUN, HALF_S, "q1", RUN)
-        make_gate(G_GATE, RUN, HALF_S, "g1", RUN)
-        make_gate(G_GATE, HALF_S, S, "g2", HALF_S)
-        make_gate(Q_GATE, HALF_S, S, "q1", RUN)
-
+        picked = keep.tile([P, HALF], F32, name="picked")
         kept = keep.tile([P, S], F32, name="kept")
         result = keep.tile([P, S], F32, name="result")
 
-        for first, end in ((0, RUN), (RUN, HALF_S), (HALF_S, S)):
-            nc.vector.tensor_tensor(
-                kept[:, first:end], cell_sb[:].indirect(entries(first, end)), gates[:, F_GATE, first:end], ALU.mult
-            )
-
-        def multiply_q_g(run):
-            cols = slice(run * RUN, (run + 1) * RUN)
-            nc.vector.tensor_tensor(result[:, cols], gates[:, Q_GATE, cols], gates[:, G_GATE, cols], ALU.mult)
-
-        def add_kept(run):
-            cols = slice(run * RUN, (run + 1) * RUN)
-            nc.vector.tensor_tensor(result[:, cols], kept[:, cols], result[:, cols], ALU.add)
+        def run_cols(run):
+            return slice(run * RUN, (run + 1) * RUN)
 
         def store(first, end):
             nc.sync.dma_start(out=out[:, first:end], in_=result[:, first:end])
 
-        multiply_q_g(0)
-        multiply_q_g(1)
-        add_kept(0)
-        add_kept(1)
-        store(0, HALF_S)
-        multiply_q_g(2)
-        multiply_q_g(3)
-        add_kept(2)
-        store(HALF_S, 3 * RUN)
-        add_kept(3)
-        store(3 * RUN, S)
+        for run in range(2):
+            for gate in (F_GATE, Q_GATE, G_GATE):
+                make_gate(gate, run * RUN, (run + 1) * RUN, "b%d_%d" % (gate, run), RUN, gates[:, gate, run_cols(run)])
+        make_gate(F_GATE, HALF, S, "b0_0", HALF, f_late[:])
+        nc.scalar.activation(picked[:], cell_sb[:].indirect(entries(HALF, S)), ACT.Copy)
+
+        for run in range(2):
+            nc.vector.tensor_tensor(
+                kept[:, run_cols(run)], cell_sb[:].indirect(entries(run * RUN, (run + 1) * RUN)),
+                gates[:, F_GATE, run_cols(run)], ALU.mult,
+            )
+        for run in range(2):
+            cols = run_cols(run)
+            nc.vector.tensor_tensor(gates[:, F_GATE, cols], gates[:, Q_GATE, cols], gates[:, G_GATE, cols], ALU.mult)
+        make_gate(G_GATE, HALF, S, "g2", HALF, gates[:, G_GATE, :])
+        make_gate(Q_GATE, HALF, S, "q2", RUN, gates[:, Q_GATE, :])
+        for run in range(2):
+            cols = run_cols(run)
+            nc.vector.tensor_tensor(result[:, cols], kept[:, cols], gates[:, F_GATE, cols], ALU.add)
+        store(0, HALF)
+        nc.vector.tensor_tensor(kept[:, HALF:S], picked[:], f_late[:], ALU.mult)
+        for run in range(2):
+            cols = run_cols(run)
+            nc.vector.tensor_tensor(gates[:, F_GATE, cols], gates[:, Q_GATE, cols], gates[:, G_GATE, cols], ALU.mult)
+        for run in range(2):
+            cols = run_cols(2 + run)
+            nc.vector.tensor_tensor(result[:, cols], kept[:, cols], gates[:, F_GATE, run_cols(run)], ALU.add)
+            store((2 + run) * RUN, (3 + run) * RUN)

@@ -20,7 +20,7 @@ RUN = 256
 F_GATE, Q_GATE, G_GATE = 0, 1, 2
 OWN = 256
 HALF = 512
-LAST_CUTS = (256, 384, 512, 768, 1024)
+LAST_CUTS = (256, 320, 512, 768, 1024)
 
 
 def tile_picked_beamcell_none_l_kernel(
@@ -138,10 +138,13 @@ def tile_picked_beamcell_none_l_kernel(
         def store(first, end):
             nc.sync.dma_start(out=out[:, first:end], in_=result[:, first:end])
 
+        for gate, run, bank_tag in (
+            (F_GATE, 0, "first"), (Q_GATE, 0, "chain_a"), (G_GATE, 0, "chain_b"),
+            (F_GATE, 1, "chain_a"), (G_GATE, 1, "chain_c"), (Q_GATE, 1, "chain_b"),
+        ):
+            make_gate(gate, run * RUN, (run + 1) * RUN, bank_tag, RUN, gates[:, gate, run_cols(run)])
         for run in range(2):
-            for gate in (F_GATE, Q_GATE, G_GATE):
-                make_gate(gate, run * RUN, (run + 1) * RUN, "b%d_%d" % (gate, run), RUN, gates[:, gate, run_cols(run)])
-        make_gate(F_GATE, HALF, S, "b0_0", HALF, f_late[:])
+            make_gate(F_GATE, (2 + run) * RUN, (3 + run) * RUN, ("chain_a", "chain_c")[run], RUN, f_late[:, run_cols(run)])
         nc.scalar.activation(picked[:], cell_sb[:].indirect(entries(HALF, S)), ACT.Copy)
 
         for run in range(2):
@@ -152,8 +155,8 @@ def tile_picked_beamcell_none_l_kernel(
         for run in range(2):
             cols = run_cols(run)
             nc.vector.tensor_tensor(gates[:, F_GATE, cols], gates[:, Q_GATE, cols], gates[:, G_GATE, cols], ALU.mult)
-        make_gate(G_GATE, HALF, S, "g2", HALF, gates[:, G_GATE, :])
-        make_gate(Q_GATE, HALF, S, "q2", RUN, gates[:, Q_GATE, :])
+        make_gate(G_GATE, HALF, S, "chain_a", HALF, gates[:, G_GATE, :])
+        make_gate(Q_GATE, HALF, S, "chain_c", RUN, gates[:, Q_GATE, :])
         for run in range(2):
             cols = run_cols(run)
             nc.vector.tensor_tensor(result[:, cols], kept[:, cols], gates[:, F_GATE, cols], ALU.add)

@@ -18,9 +18,11 @@ ALU = mybir.AluOpType
 P = 128
 RUN = 256
 F_GATE, Q_GATE, G_GATE = 0, 1, 2
-OWN = 256
 HALF = 512
-LAST_CUTS = (256, 320, 512, 768, 1024)
+EARLY_OWN = 384
+STEP = (640, 896)
+LAST_LOADS = (0, 1024, 1664, 2048)
+FUSED = 640
 
 
 def tile_picked_beamcell_none_l_kernel(
@@ -39,10 +41,16 @@ def tile_picked_beamcell_none_l_kernel(
         nc.scalar.activation(warm[:, 1:2], warm[:, 0:1], ACT.Sigmoid)
 
         raw = [keep.tile([P, T], F32, name="raw_%d" % t) for t in range(4)]
+        rounded = keep.tile([P, T], BF16, name="rounded", align_bytes=64)
         offsets = keep.tile([P, S // 16], U16, name="offsets")
         w_codes = keep.tile([P, 3, N], U32, name="w_codes", align_bytes=64)
         cell_sb = keep.tile([P, T], F32, name="cell_sb")
         x_rows = xT.rearrange("(p t) c -> p t c", t=4)
+
+        def load_codes(gate, words):
+            nc.sync.dma_start(
+                out=w_codes[:, gate, :].bitcast(I32), in_=words[0].rearrange("p n t -> p (n t)").bitcast(I32)
+            )
 
         nc.sync.dma_start(out=raw[0][:], in_=x_rows[:, 0, :])
         nc.sync.dma_start(offsets[:], offs)
@@ -55,33 +63,30 @@ def tile_picked_beamcell_none_l_kernel(
                 out=w_scales[32 * quadrant:32 * quadrant + 4, :].bitcast(I32),
                 in_=w_scales[4 * quadrant:4 * quadrant + 4, :].bitcast(I32),
             )
-        nc.sync.dma_start(out=raw[3][:], in_=x_rows[:, 3, :])
-        for gate, words in enumerate((w1_words, w2_words, w3_words)):
-            nc.sync.dma_start(
-                out=w_codes[:, gate, :].bitcast(I32), in_=words[0].rearrange("p n t -> p (n t)").bitcast(I32)
-            )
+        for first, end in zip(LAST_LOADS[:-1], LAST_LOADS[1:]):
+            nc.sync.dma_start(out=raw[3][:, first:end], in_=x_rows[:, 3, first:end])
+        load_codes(F_GATE, w1_words)
+        load_codes(Q_GATE, w2_words)
         nc.sync.dma_start(out=cell_sb[:], in_=cell)
+        load_codes(G_GATE, w3_words)
 
         def entries(first, end):
             return offsets[:, first // 16:end // 16]
 
         woven = keep.tile([P, S, 4], BF16, name="woven", align_bytes=64)
-        planes = [keep.tile([P, 2, S - OWN], BF16, name="planes_%d" % h, align_bytes=64) for h in range(2)]
+        planes = [keep.tile([P, 2, S], BF16, name="planes_%d" % pair, align_bytes=64) for pair in range(2)]
         x_codes = keep.tile([P, S], U32, name="x_codes", align_bytes=64)
         x_scales = keep.tile([P, S], U8, name="x_scales", align_bytes=64)
 
-        def gather_own(t):
-            nc.vector.tensor_copy(woven[:, 0:OWN, t], raw[t][:].indirect(entries(0, OWN)))
+        def gather_woven(t, first, end):
+            nc.vector.tensor_copy(woven[:, first:end, t], raw[t][:].indirect(entries(first, end)))
 
         def gather_plane(t, first, end):
-            nc.scalar.activation(
-                planes[t // 2][:, t % 2, first - OWN:end - OWN], raw[t][:].indirect(entries(first, end)), ACT.Copy
-            )
+            nc.scalar.activation(planes[t // 2][:, t % 2, first:end], raw[t][:].indirect(entries(first, end)), ACT.Copy)
 
         def place(pair, first, end):
             nc.vector.tensor_copy(
-                woven[:, first:end, 2 * pair:2 * pair + 2],
-                planes[pair][:, :, first - OWN:end - OWN].rearrange("p t n -> p n t"),
+                woven[:, first:end, 2 * pair:2 * pair + 2], planes[pair][:, :, first:end].rearrange("p t n -> p n t")
             )
 
         def quantise(run):
@@ -92,27 +97,43 @@ def tile_picked_beamcell_none_l_kernel(
                 in_=woven[:, cols, :].rearrange("p n t -> p (n t)"),
             )
 
-        for t in range(3):
-            gather_own(t)
-            gather_plane(t, OWN, S)
-            if t == 1:
-                place(0, OWN, S)
-        gather_own(3)
-        for first, end in zip(LAST_CUTS[:-1], LAST_CUTS[1:]):
+        def round_on_gpsimd(first, end):
+            nc.gpsimd.tensor_scalar(rounded[:, first:end], raw[3][:, first:end], 1.0, 0.0, ALU.mult, ALU.add)
+
+        gather_woven(0, 0, EARLY_OWN)
+        gather_plane(0, EARLY_OWN, S)
+        gather_woven(1, 0, EARLY_OWN)
+        for first, end in ((EARLY_OWN, 704), (704, S)):
+            gather_plane(1, first, end)
+            place(0, first, end)
+
+        gather_woven(2, 0, RUN)
+        gather_woven(2, STEP[0], STEP[1])
+        gather_plane(2, RUN, STEP[0])
+        gather_plane(2, STEP[1], S)
+        round_on_gpsimd(0, 256)
+        nc.scalar.copy(rounded[:, 256:LAST_LOADS[1]], raw[3][:, 256:LAST_LOADS[1]])
+        nc.vector.tensor_copy(rounded[:, LAST_LOADS[1]:LAST_LOADS[2]], raw[3][:, LAST_LOADS[1]:LAST_LOADS[2]])
+        round_on_gpsimd(LAST_LOADS[2], T)
+
+        gather_woven(3, 0, RUN)
+        for first, end in ((RUN, 320), (320, STEP[0]), (STEP[1], S)):
             gather_plane(3, first, end)
-        place(1, LAST_CUTS[0], LAST_CUTS[1])
+        nc.scalar.activation(woven[:, STEP[0]:STEP[1], 3], rounded[:].indirect(entries(STEP[0], STEP[1])), ACT.Copy)
+        place(1, RUN, 320)
         quantise(0)
-        place(1, LAST_CUTS[1], LAST_CUTS[2])
-        place(1, LAST_CUTS[2], LAST_CUTS[3])
+        place(1, 320, 2 * RUN)
+        place(1, 2 * RUN, STEP[0])
         quantise(1)
-        place(1, LAST_CUTS[3], LAST_CUTS[4])
+        place(1, STEP[1], S)
         quantise(2)
         quantise(3)
 
-        gates = keep.tile([P, 3, HALF], F32, name="gates")
-        f_late = keep.tile([P, HALF], F32, name="f_late")
+        f_gate = keep.tile([P, S], F32, name="f_gate")
+        g_gate = keep.tile([P, S], F32, name="g_gate")
+        q_gate = keep.tile([P, HALF], F32, name="q_gate")
 
-        def make_gate(gate, first, end, tag, width, dest):
+        def make_gate(gate, first, end, tag, cuts, dest):
             bank = psum.tile([P, end - first], F32, name="bank_%d_%d" % (gate, first), tag=tag)
             nc.tensor.matmul_mx(
                 out=bank[:],
@@ -123,49 +144,52 @@ def tile_picked_beamcell_none_l_kernel(
                 start=True,
                 stop=True,
             )
-            for lo in range(0, end - first, width):
-                nc.scalar.activation(
-                    dest[:, lo:lo + width], bank[:, lo:lo + width], ACT.Tanh if gate == G_GATE else ACT.Sigmoid
-                )
+            for lo, hi in zip(cuts[:-1], cuts[1:]):
+                nc.scalar.activation(dest[:, lo:hi], bank[:, lo:hi], ACT.Tanh if gate == G_GATE else ACT.Sigmoid)
 
-        picked = keep.tile([P, HALF], F32, name="picked")
+        picked = keep.tile([P, S - FUSED], F32, name="picked")
         kept = keep.tile([P, S], F32, name="kept")
         result = keep.tile([P, S], F32, name="result")
+        whole = (0, RUN)
 
-        def run_cols(run):
-            return slice(run * RUN, (run + 1) * RUN)
+        def multiply_q_g(first, end):
+            nc.vector.tensor_tensor(
+                result[:, first:end], q_gate[:, first % HALF:first % HALF + end - first], g_gate[:, first:end], ALU.mult
+            )
+
+        def add_kept(first, end):
+            nc.vector.tensor_tensor(result[:, first:end], kept[:, first:end], result[:, first:end], ALU.add)
 
         def store(first, end):
             nc.sync.dma_start(out=out[:, first:end], in_=result[:, first:end])
 
-        for gate, run, bank_tag in (
-            (F_GATE, 0, "first"), (Q_GATE, 0, "chain_a"), (G_GATE, 0, "chain_b"),
-            (F_GATE, 1, "chain_a"), (G_GATE, 1, "chain_c"), (Q_GATE, 1, "chain_b"),
-        ):
-            make_gate(gate, run * RUN, (run + 1) * RUN, bank_tag, RUN, gates[:, gate, run_cols(run)])
-        for run in range(2):
-            make_gate(F_GATE, (2 + run) * RUN, (3 + run) * RUN, ("chain_a", "chain_c")[run], RUN, f_late[:, run_cols(run)])
-        nc.scalar.activation(picked[:], cell_sb[:].indirect(entries(HALF, S)), ACT.Copy)
+        make_gate(F_GATE, 0, RUN, "a", whole, f_gate[:, 0:RUN])
+        make_gate(Q_GATE, 0, RUN, "b", whole, q_gate[:, 0:RUN])
+        make_gate(Q_GATE, RUN, HALF, "c", whole, q_gate[:, RUN:HALF])
+        make_gate(F_GATE, RUN, HALF, "a", whole, f_gate[:, RUN:HALF])
+        make_gate(F_GATE, HALF, 3 * RUN, "d", whole, f_gate[:, HALF:3 * RUN])
+        make_gate(F_GATE, 3 * RUN, S, "e", whole, f_gate[:, 3 * RUN:S])
+        nc.scalar.activation(picked[:], cell_sb[:].indirect(entries(FUSED, S)), ACT.Copy)
+        make_gate(G_GATE, 0, RUN, "f", whole, g_gate[:, 0:RUN])
+        make_gate(G_GATE, RUN, HALF, "g", whole, g_gate[:, RUN:HALF])
+        make_gate(G_GATE, HALF, S, "h", (0, HALF), g_gate[:, HALF:S])
 
-        for run in range(2):
+        for first, end in ((0, RUN), (RUN, HALF), (HALF, FUSED)):
             nc.vector.tensor_tensor(
-                kept[:, run_cols(run)], cell_sb[:].indirect(entries(run * RUN, (run + 1) * RUN)),
-                gates[:, F_GATE, run_cols(run)], ALU.mult,
+                kept[:, first:end], cell_sb[:].indirect(entries(first, end)), f_gate[:, first:end], ALU.mult
             )
-        for run in range(2):
-            cols = run_cols(run)
-            nc.vector.tensor_tensor(gates[:, F_GATE, cols], gates[:, Q_GATE, cols], gates[:, G_GATE, cols], ALU.mult)
-        make_gate(G_GATE, HALF, S, "chain_a", HALF, gates[:, G_GATE, :])
-        make_gate(Q_GATE, HALF, S, "chain_c", RUN, gates[:, Q_GATE, :])
-        for run in range(2):
-            cols = run_cols(run)
-            nc.vector.tensor_tensor(result[:, cols], kept[:, cols], gates[:, F_GATE, cols], ALU.add)
+        nc.vector.tensor_tensor(kept[:, FUSED:S], picked[:], f_gate[:, FUSED:S], ALU.mult)
+        multiply_q_g(0, RUN)
+        multiply_q_g(RUN, HALF)
+        make_gate(Q_GATE, HALF, S, "f", (0, RUN, 384, HALF), q_gate[:])
+        add_kept(0, RUN)
+        add_kept(RUN, HALF)
         store(0, HALF)
-        nc.vector.tensor_tensor(kept[:, HALF:S], picked[:], f_late[:], ALU.mult)
-        for run in range(2):
-            cols = run_cols(run)
-            nc.vector.tensor_tensor(gates[:, F_GATE, cols], gates[:, Q_GATE, cols], gates[:, G_GATE, cols], ALU.mult)
-        for run in range(2):
-            cols = run_cols(2 + run)
-            nc.vector.tensor_tensor(result[:, cols], kept[:, cols], gates[:, F_GATE, run_cols(run)], ALU.add)
-            store((2 + run) * RUN, (3 + run) * RUN)
+        multiply_q_g(HALF, 3 * RUN)
+        multiply_q_g(3 * RUN, 896)
+        add_kept(HALF, 3 * RUN)
+        store(HALF, 3 * RUN)
+        multiply_q_g(896, S)
+        add_kept(3 * RUN, 896)
+        add_kept(896, S)
+        store(3 * RUN, S)

@@ -22,7 +22,7 @@ HALF = 512
 EARLY_OWN = 384
 STEP = (640, 896)
 LAST_LOADS = (0, 1024, 1664, 2048)
-FUSED = 640
+FUSED = 768
 
 
 def tile_picked_beamcell_none_l_kernel(
@@ -181,15 +181,13 @@ def tile_picked_beamcell_none_l_kernel(
         nc.vector.tensor_tensor(kept[:, FUSED:S], picked[:], f_gate[:, FUSED:S], ALU.mult)
         multiply_q_g(0, RUN)
         multiply_q_g(RUN, HALF)
-        make_gate(Q_GATE, HALF, S, "f", (0, RUN, 384, HALF), q_gate[:])
+        make_gate(Q_GATE, HALF, S, "f", (0, RUN, HALF), q_gate[:])
         add_kept(0, RUN)
         add_kept(RUN, HALF)
         store(0, HALF)
         multiply_q_g(HALF, 3 * RUN)
-        multiply_q_g(3 * RUN, 896)
+        multiply_q_g(3 * RUN, S)
         add_kept(HALF, 3 * RUN)
         store(HALF, 3 * RUN)
-        multiply_q_g(896, S)
-        add_kept(3 * RUN, 896)
-        add_kept(896, S)
+        add_kept(3 * RUN, S)
         store(3 * RUN, S)

@@ -20,8 +20,8 @@ RUN = 256
 F_GATE, Q_GATE, G_GATE = 0, 1, 2
 HALF = 512
 EARLY_OWN = 384
-STEP = (640, 896)
-LAST_LOADS = (0, 1024, 1664, 2048)
+STEP = (640, 1024)
+LAST_LOADS = (0, 1152, 1664, 2048)
 FUSED = 768
 
 
@@ -52,23 +52,27 @@ def tile_picked_beamcell_none_l_kernel(
                 out=w_codes[:, gate, :].bitcast(I32), in_=words[0].rearrange("p n t -> p (n t)").bitcast(I32)
             )
 
+        def move_scales(quadrant):
+            nc.sync.dma_start(
+                out=w_scales[32 * quadrant:32 * quadrant + 4, :].bitcast(I32),
+                in_=w_scales[4 * quadrant:4 * quadrant + 4, :].bitcast(I32),
+            )
+
         nc.sync.dma_start(out=raw[0][:], in_=x_rows[:, 0, :])
         nc.sync.dma_start(offsets[:], offs)
         for gate, scales in enumerate((w1_scales, w2_scales, w3_scales)):
             nc.sync.dma_start(out=w_scales[0:16, gate * N:(gate + 1) * N].bitcast(I32), in_=scales[0].bitcast(I32))
         nc.sync.dma_start(out=raw[1][:], in_=x_rows[:, 1, :])
         nc.sync.dma_start(out=raw[2][:], in_=x_rows[:, 2, :])
-        for quadrant in range(1, 4):
-            nc.sync.dma_start(
-                out=w_scales[32 * quadrant:32 * quadrant + 4, :].bitcast(I32),
-                in_=w_scales[4 * quadrant:4 * quadrant + 4, :].bitcast(I32),
-            )
+        move_scales(1)
+        move_scales(2)
         for first, end in zip(LAST_LOADS[:-1], LAST_LOADS[1:]):
             nc.sync.dma_start(out=raw[3][:, first:end], in_=x_rows[:, 3, first:end])
         load_codes(F_GATE, w1_words)
         load_codes(Q_GATE, w2_words)
-        nc.sync.dma_start(out=cell_sb[:], in_=cell)
         load_codes(G_GATE, w3_words)
+        move_scales(3)
+        nc.sync.dma_start(out=cell_sb[:], in_=cell)
 
         def entries(first, end):
             return offsets[:, first // 16:end // 16]
@@ -110,14 +114,13 @@ def tile_picked_beamcell_none_l_kernel(
         gather_woven(2, 0, RUN)
         gather_woven(2, STEP[0], STEP[1])
         gather_plane(2, RUN, STEP[0])
-        gather_plane(2, STEP[1], S)
         round_on_gpsimd(0, 256)
         nc.scalar.copy(rounded[:, 256:LAST_LOADS[1]], raw[3][:, 256:LAST_LOADS[1]])
         nc.vector.tensor_copy(rounded[:, LAST_LOADS[1]:LAST_LOADS[2]], raw[3][:, LAST_LOADS[1]:LAST_LOADS[2]])
         round_on_gpsimd(LAST_LOADS[2], T)
 
         gather_woven(3, 0, RUN)
-        for first, end in ((RUN, 320), (320, STEP[0]), (STEP[1], S)):
+        for first, end in ((RUN, 320), (320, STEP[0])):
             gather_plane(3, first, end)
         nc.scalar.activation(woven[:, STEP[0]:STEP[1], 3], rounded[:].indirect(entries(STEP[0], STEP[1])), ACT.Copy)
         place(1, RUN, 320)
@@ -125,7 +128,6 @@ def tile_picked_beamcell_none_l_kernel(
         place(1, 320, 2 * RUN)
         place(1, 2 * RUN, STEP[0])
         quantise(1)
-        place(1, STEP[1], S)
         quantise(2)
         quantise(3)
 
@@ -152,42 +154,44 @@ def tile_picked_beamcell_none_l_kernel(
         result = keep.tile([P, S], F32, name="result")
         whole = (0, RUN)
 
-        def multiply_q_g(first, end):
+        def multiply_q_g(dest, first, end):
             nc.vector.tensor_tensor(
-                result[:, first:end], q_gate[:, first % HALF:first % HALF + end - first], g_gate[:, first:end], ALU.mult
+                dest[:, first:end], q_gate[:, first % HALF:first % HALF + end - first], g_gate[:, first:end], ALU.mult
             )
 
-        def add_kept(first, end):
-            nc.vector.tensor_tensor(result[:, first:end], kept[:, first:end], result[:, first:end], ALU.add)
+        def add_kept(product, first, end):
+            nc.vector.tensor_tensor(result[:, first:end], kept[:, first:end], product[:, first:end], ALU.add)
+
+        def fused(first, end):
+            nc.vector.tensor_tensor(
+                kept[:, first:end], cell_sb[:].indirect(entries(first, end)), f_gate[:, first:end], ALU.mult
+            )
 
         def store(first, end):
             nc.sync.dma_start(out=out[:, first:end], in_=result[:, first:end])
 
-        make_gate(F_GATE, 0, RUN, "a", whole, f_gate[:, 0:RUN])
-        make_gate(Q_GATE, 0, RUN, "b", whole, q_gate[:, 0:RUN])
-        make_gate(Q_GATE, RUN, HALF, "c", whole, q_gate[:, RUN:HALF])
-        make_gate(F_GATE, RUN, HALF, "a", whole, f_gate[:, RUN:HALF])
-        make_gate(F_GATE, HALF, 3 * RUN, "d", whole, f_gate[:, HALF:3 * RUN])
-        make_gate(F_GATE, 3 * RUN, S, "e", whole, f_gate[:, 3 * RUN:S])
+        for run in range(2):
+            cols = slice(run * RUN, (run + 1) * RUN)
+            for gate, dest in ((F_GATE, f_gate), (Q_GATE, q_gate), (G_GATE, g_gate)):
+                make_gate(gate, cols.start, cols.stop, "b%d%d" % (gate, run), whole, dest[:, cols])
+        make_gate(F_GATE, HALF, 3 * RUN, "b00", whole, f_gate[:, HALF:3 * RUN])
+        make_gate(F_GATE, 3 * RUN, S, "b10", whole, f_gate[:, 3 * RUN:S])
         nc.scalar.activation(picked[:], cell_sb[:].indirect(entries(FUSED, S)), ACT.Copy)
-        make_gate(G_GATE, 0, RUN, "f", whole, g_gate[:, 0:RUN])
-        make_gate(G_GATE, RUN, HALF, "g", whole, g_gate[:, RUN:HALF])
-        make_gate(G_GATE, HALF, S, "h", (0, HALF), g_gate[:, HALF:S])
+        make_gate(G_GATE, HALF, S, "g23", (0, HALF), g_gate[:, HALF:S])
 
-        for first, end in ((0, RUN), (RUN, HALF), (HALF, FUSED)):
-            nc.vector.tensor_tensor(
-                kept[:, first:end], cell_sb[:].indirect(entries(first, end)), f_gate[:, first:end], ALU.mult
-            )
-        nc.vector.tensor_tensor(kept[:, FUSED:S], picked[:], f_gate[:, FUSED:S], ALU.mult)
-        multiply_q_g(0, RUN)
-        multiply_q_g(RUN, HALF)
-        make_gate(Q_GATE, HALF, S, "f", (0, RUN, HALF), q_gate[:])
-        add_kept(0, RUN)
-        add_kept(RUN, HALF)
+        fused(0, RUN)
+        fused(RUN, HALF)
+        multiply_q_g(f_gate, 0, RUN)
+        multiply_q_g(f_gate, RUN, HALF)
+        make_gate(Q_GATE, HALF, S, "q23", (0, RUN, HALF), q_gate[:])
+        add_kept(f_gate, 0, RUN)
+        add_kept(f_gate, RUN, HALF)
         store(0, HALF)
-        multiply_q_g(HALF, 3 * RUN)
-        multiply_q_g(3 * RUN, S)
-        add_kept(HALF, 3 * RUN)
+        fused(HALF, FUSED)
+        nc.vector.tensor_tensor(kept[:, FUSED:S], picked[:], f_gate[:, FUSED:S], ALU.mult)
+        multiply_q_g(result, HALF, 3 * RUN)
+        multiply_q_g(result, 3 * RUN, S)
+        add_kept(result, HALF, 3 * RUN)
         store(HALF, 3 * RUN)
-        add_kept(3 * RUN, S)
+        add_kept(result, 3 * RUN, S)
         store(3 * RUN, S)

@@ -93,8 +93,8 @@ def tile_picked_beamcell_none_l_kernel(
                 woven[:, first:end, 2 * pair:2 * pair + 2], planes[pair][:, :, first:end].rearrange("p t n -> p n t")
             )
 
-        def quantise(run):
-            cols = slice(run * RUN, (run + 1) * RUN)
+        def quantise(first, end):
+            cols = slice(first, end)
             nc.vector.quantize_mx(
                 out=x_codes[:, cols].bitcast(FP8X4),
                 scales=x_scales[:, cols],
@@ -124,74 +124,62 @@ def tile_picked_beamcell_none_l_kernel(
             gather_plane(3, first, end)
         nc.scalar.activation(woven[:, STEP[0]:STEP[1], 3], rounded[:].indirect(entries(STEP[0], STEP[1])), ACT.Copy)
         place(1, RUN, 320)
-        quantise(0)
+        quantise(0, RUN)
         place(1, 320, 2 * RUN)
         place(1, 2 * RUN, STEP[0])
-        quantise(1)
-        quantise(2)
-        quantise(3)
+        quantise(RUN, HALF)
+        quantise(HALF, S)
 
-        f_gate = keep.tile([P, S], F32, name="f_gate")
+        early = keep.tile([P, 5 * RUN], F32, name="early")
+        late = keep.tile([P, 2, HALF], F32, name="late")
         g_gate = keep.tile([P, S], F32, name="g_gate")
-        q_gate = keep.tile([P, HALF], F32, name="q_gate")
-
-        def make_gate(gate, first, end, tag, cuts, dest):
-            bank = psum.tile([P, end - first], F32, name="bank_%d_%d" % (gate, first), tag=tag)
-            nc.tensor.matmul_mx(
-                out=bank[:],
-                lhsT=w_codes[:, gate, :].bitcast(FP8X4),
-                lhsT_scale=w_scales[:, gate * N:(gate + 1) * N],
-                rhs=x_codes[:, first:end].bitcast(FP8X4),
-                rhs_scale=x_scales[:, first:end],
-                start=True,
-                stop=True,
-            )
-            for lo, hi in zip(cuts[:-1], cuts[1:]):
-                nc.scalar.activation(dest[:, lo:hi], bank[:, lo:hi], ACT.Tanh if gate == G_GATE else ACT.Sigmoid)
-
         picked = keep.tile([P, S - FUSED], F32, name="picked")
         kept = keep.tile([P, S], F32, name="kept")
         result = keep.tile([P, S], F32, name="result")
-        whole = (0, RUN)
 
-        def multiply_q_g(dest, first, end):
+        def make_gates(name, products, dest, func):
+            bank = psum.tile([P, sum(end - first for gate, first, end in products)], F32, name=name)
+            at = 0
+            for gate, first, end in products:
+                nc.tensor.matmul_mx(
+                    out=bank[:, at:at + end - first],
+                    lhsT=w_codes[:, gate, :].bitcast(FP8X4),
+                    lhsT_scale=w_scales[:, gate * N:(gate + 1) * N],
+                    rhs=x_codes[:, first:end].bitcast(FP8X4),
+                    rhs_scale=x_scales[:, first:end],
+                    start=True,
+                    stop=True,
+                )
+                at = at + end - first
+            nc.scalar.activation(dest, bank[:], func)
+
+        make_gates("fq0", ((F_GATE, 0, RUN), (Q_GATE, 0, RUN)), early[:, RUN:3 * RUN], ACT.Sigmoid)
+        make_gates("g0", ((G_GATE, 0, RUN),), g_gate[:, 0:RUN], ACT.Tanh)
+        make_gates("f1", ((F_GATE, RUN, HALF),), early[:, 4 * RUN:5 * RUN], ACT.Sigmoid)
+        make_gates("q1", ((Q_GATE, RUN, HALF),), early[:, 3 * RUN:4 * RUN], ACT.Sigmoid)
+        make_gates("g1", ((G_GATE, RUN, HALF),), g_gate[:, RUN:HALF], ACT.Tanh)
+        make_gates("f23", ((F_GATE, HALF, S),), late[:, F_GATE, :], ACT.Sigmoid)
+        make_gates("g23", ((G_GATE, HALF, S),), g_gate[:, HALF:S], ACT.Tanh)
+        make_gates("q23", ((Q_GATE, HALF, S),), late[:, Q_GATE, :], ACT.Sigmoid)
+        nc.scalar.activation(picked[:], cell_sb[:].indirect(entries(FUSED, S)), ACT.Copy)
+
+        def fused(first, f_cols):
             nc.vector.tensor_tensor(
-                dest[:, first:end], q_gate[:, first % HALF:first % HALF + end - first], g_gate[:, first:end], ALU.mult
-            )
-
-        def add_kept(product, first, end):
-            nc.vector.tensor_tensor(result[:, first:end], kept[:, first:end], product[:, first:end], ALU.add)
-
-        def fused(first, end):
-            nc.vector.tensor_tensor(
-                kept[:, first:end], cell_sb[:].indirect(entries(first, end)), f_gate[:, first:end], ALU.mult
+                kept[:, first:first + RUN], cell_sb[:].indirect(entries(first, first + RUN)), f_cols, ALU.mult
             )
 
         def store(first, end):
             nc.sync.dma_start(out=out[:, first:end], in_=result[:, first:end])
 
-        for run in range(2):
-            cols = slice(run * RUN, (run + 1) * RUN)
-            for gate, dest in ((F_GATE, f_gate), (Q_GATE, q_gate), (G_GATE, g_gate)):
-                make_gate(gate, cols.start, cols.stop, "b%d%d" % (gate, run), whole, dest[:, cols])
-        make_gate(F_GATE, HALF, 3 * RUN, "b00", whole, f_gate[:, HALF:3 * RUN])
-        make_gate(F_GATE, 3 * RUN, S, "b10", whole, f_gate[:, 3 * RUN:S])
-        nc.scalar.activation(picked[:], cell_sb[:].indirect(entries(FUSED, S)), ACT.Copy)
-        make_gate(G_GATE, HALF, S, "g23", (0, HALF), g_gate[:, HALF:S])
-
-        fused(0, RUN)
-        fused(RUN, HALF)
-        multiply_q_g(f_gate, 0, RUN)
-        multiply_q_g(f_gate, RUN, HALF)
-        make_gate(Q_GATE, HALF, S, "q23", (0, RUN, HALF), q_gate[:])
-        add_kept(f_gate, 0, RUN)
-        add_kept(f_gate, RUN, HALF)
+        fused(0, early[:, RUN:2 * RUN])
+        fused(RUN, early[:, 4 * RUN:5 * RUN])
+        nc.vector.tensor_tensor(early[:, 0:HALF], early[:, 2 * RUN:4 * RUN], g_gate[:, 0:HALF], ALU.mult)
+        fused(HALF, late[:, F_GATE, 0:RUN])
+        nc.vector.tensor_tensor(result[:, 0:HALF], kept[:, 0:HALF], early[:, 0:HALF], ALU.add)
         store(0, HALF)
-        fused(HALF, FUSED)
-        nc.vector.tensor_tensor(kept[:, FUSED:S], picked[:], f_gate[:, FUSED:S], ALU.mult)
-        multiply_q_g(result, HALF, 3 * RUN)
-        multiply_q_g(result, 3 * RUN, S)
-        add_kept(result, HALF, 3 * RUN)
-        store(HALF, 3 * RUN)
-        add_kept(result, 3 * RUN, S)
-        store(3 * RUN, S)
+        nc.vector.tensor_tensor(result[:, HALF:S], late[:, Q_GATE, :], g_gate[:, HALF:S], ALU.mult)
+        nc.vector.tensor_tensor(kept[:, FUSED:S], picked[:], late[:, F_GATE, RUN:HALF], ALU.mult)
+        for first in (HALF, FUSED):
+            cols = slice(first, first + RUN)
+            nc.vector.tensor_tensor(result[:, cols], kept[:, cols], result[:, cols], ALU.add)
+            store(first, first + RUN)

@@ -21,7 +21,8 @@ F_GATE, Q_GATE, G_GATE = 0, 1, 2
 HALF = 512
 EARLY_OWN = 384
 STEP = (640, 1024)
-LAST_LOADS = (0, 1152, 1664, 2048)
+LAST_LOADS = (0, 1536, 2048)
+ROUND_ON_SCALAR = 448
 FUSED = 768
 
 
@@ -65,13 +66,13 @@ def tile_picked_beamcell_none_l_kernel(
         nc.sync.dma_start(out=raw[1][:], in_=x_rows[:, 1, :])
         nc.sync.dma_start(out=raw[2][:], in_=x_rows[:, 2, :])
         move_scales(1)
-        move_scales(2)
         for first, end in zip(LAST_LOADS[:-1], LAST_LOADS[1:]):
             nc.sync.dma_start(out=raw[3][:, first:end], in_=x_rows[:, 3, first:end])
         load_codes(F_GATE, w1_words)
         load_codes(Q_GATE, w2_words)
         load_codes(G_GATE, w3_words)
-        move_scales(3)
+        for quadrant in range(2, 4):
+            move_scales(quadrant)
         nc.sync.dma_start(out=cell_sb[:], in_=cell)
 
         def entries(first, end):
@@ -112,12 +113,12 @@ def tile_picked_beamcell_none_l_kernel(
             place(0, first, end)
 
         gather_woven(2, 0, RUN)
-        gather_woven(2, STEP[0], STEP[1])
+        gather_plane(2, STEP[0], STEP[1])
         gather_plane(2, RUN, STEP[0])
-        round_on_gpsimd(0, 256)
-        nc.scalar.copy(rounded[:, 256:LAST_LOADS[1]], raw[3][:, 256:LAST_LOADS[1]])
-        nc.vector.tensor_copy(rounded[:, LAST_LOADS[1]:LAST_LOADS[2]], raw[3][:, LAST_LOADS[1]:LAST_LOADS[2]])
-        round_on_gpsimd(LAST_LOADS[2], T)
+        nc.vector.tensor_copy(woven[:, STEP[0]:STEP[1], 2], planes[1][:, 0, STEP[0]:STEP[1]])
+        nc.scalar.copy(rounded[:, 0:ROUND_ON_SCALAR], raw[3][:, 0:ROUND_ON_SCALAR])
+        nc.vector.tensor_copy(rounded[:, ROUND_ON_SCALAR:LAST_LOADS[1]], raw[3][:, ROUND_ON_SCALAR:LAST_LOADS[1]])
+        round_on_gpsimd(LAST_LOADS[1], T)
 
         gather_woven(3, 0, RUN)
         for first, end in ((RUN, 320), (320, STEP[0])):
@@ -153,10 +154,10 @@ def tile_picked_beamcell_none_l_kernel(
                 at = at + end - first
             nc.scalar.activation(dest, bank[:], func)
 
-        make_gates("fq0", ((F_GATE, 0, RUN), (Q_GATE, 0, RUN)), early[:, RUN:3 * RUN], ACT.Sigmoid)
+        make_gates("q0", ((Q_GATE, 0, RUN),), early[:, 2 * RUN:3 * RUN], ACT.Sigmoid)
         make_gates("g0", ((G_GATE, 0, RUN),), g_gate[:, 0:RUN], ACT.Tanh)
-        make_gates("f1", ((F_GATE, RUN, HALF),), early[:, 4 * RUN:5 * RUN], ACT.Sigmoid)
-        make_gates("q1", ((Q_GATE, RUN, HALF),), early[:, 3 * RUN:4 * RUN], ACT.Sigmoid)
+        make_gates("f0", ((F_GATE, 0, RUN),), early[:, RUN:2 * RUN], ACT.Sigmoid)
+        make_gates("qf1", ((Q_GATE, RUN, HALF), (F_GATE, RUN, HALF)), early[:, 3 * RUN:5 * RUN], ACT.Sigmoid)
         make_gates("g1", ((G_GATE, RUN, HALF),), g_gate[:, RUN:HALF], ACT.Tanh)
         make_gates("f23", ((F_GATE, HALF, S),), late[:, F_GATE, :], ACT.Sigmoid)
         make_gates("g23", ((G_GATE, HALF, S),), g_gate[:, HALF:S], ACT.Tanh)
@@ -171,9 +172,10 @@ def tile_picked_beamcell_none_l_kernel(
         def store(first, end):
             nc.sync.dma_start(out=out[:, first:end], in_=result[:, first:end])
 
+        nc.vector.tensor_tensor(early[:, 0:RUN], early[:, 2 * RUN:3 * RUN], g_gate[:, 0:RUN], ALU.mult)
         fused(0, early[:, RUN:2 * RUN])
         fused(RUN, early[:, 4 * RUN:5 * RUN])
-        nc.vector.tensor_tensor(early[:, 0:HALF], early[:, 2 * RUN:4 * RUN], g_gate[:, 0:HALF], ALU.mult)
+        nc.vector.tensor_tensor(early[:, RUN:HALF], early[:, 3 * RUN:4 * RUN], g_gate[:, RUN:HALF], ALU.mult)
         fused(HALF, late[:, F_GATE, 0:RUN])
         nc.vector.tensor_tensor(result[:, 0:HALF], kept[:, 0:HALF], early[:, 0:HALF], ALU.add)
         store(0, HALF)

@@ -132,37 +132,44 @@ def tile_picked_beamcell_none_l_kernel(
         quantise(HALF, S)
 
         early = keep.tile([P, 5 * RUN], F32, name="early")
-        late = keep.tile([P, 2, HALF], F32, name="late")
+        f_late = keep.tile([P, HALF], F32, name="f_late")
         g_gate = keep.tile([P, S], F32, name="g_gate")
         picked = keep.tile([P, S - FUSED], F32, name="picked")
         kept = keep.tile([P, S], F32, name="kept")
         result = keep.tile([P, S], F32, name="result")
 
-        def make_gates(name, products, dest, func):
-            bank = psum.tile([P, sum(end - first for gate, first, end in products)], F32, name=name)
-            at = 0
-            for gate, first, end in products:
-                nc.tensor.matmul_mx(
-                    out=bank[:, at:at + end - first],
-                    lhsT=w_codes[:, gate, :].bitcast(FP8X4),
-                    lhsT_scale=w_scales[:, gate * N:(gate + 1) * N],
-                    rhs=x_codes[:, first:end].bitcast(FP8X4),
-                    rhs_scale=x_scales[:, first:end],
-                    start=True,
-                    stop=True,
-                )
-                at = at + end - first
-            nc.scalar.activation(dest, bank[:], func)
+        def stretch(place):
+            return early[:, place * RUN:(place + 1) * RUN]
 
-        make_gates("q0", ((Q_GATE, 0, RUN),), early[:, 2 * RUN:3 * RUN], ACT.Sigmoid)
-        make_gates("g0", ((G_GATE, 0, RUN),), g_gate[:, 0:RUN], ACT.Tanh)
-        make_gates("f0", ((F_GATE, 0, RUN),), early[:, RUN:2 * RUN], ACT.Sigmoid)
-        make_gates("qf1", ((Q_GATE, RUN, HALF), (F_GATE, RUN, HALF)), early[:, 3 * RUN:5 * RUN], ACT.Sigmoid)
-        make_gates("g1", ((G_GATE, RUN, HALF),), g_gate[:, RUN:HALF], ACT.Tanh)
-        make_gates("f23", ((F_GATE, HALF, S),), late[:, F_GATE, :], ACT.Sigmoid)
-        make_gates("g23", ((G_GATE, HALF, S),), g_gate[:, HALF:S], ACT.Tanh)
-        make_gates("q23", ((Q_GATE, HALF, S),), late[:, Q_GATE, :], ACT.Sigmoid)
+        def make_gate(gate, first, bank_tag, dests):
+            width = sum(dest.shape[1] for dest in dests)
+            bank = psum.tile([P, width], F32, name="bank_%d_%d" % (gate, first), tag=bank_tag)
+            nc.tensor.matmul_mx(
+                out=bank[:],
+                lhsT=w_codes[:, gate, :].bitcast(FP8X4),
+                lhsT_scale=w_scales[:, gate * N:(gate + 1) * N],
+                rhs=x_codes[:, first:first + width].bitcast(FP8X4),
+                rhs_scale=x_scales[:, first:first + width],
+                start=True,
+                stop=True,
+            )
+            at = 0
+            for dest in dests:
+                nc.scalar.activation(
+                    dest, bank[:, at:at + dest.shape[1]], ACT.Tanh if gate == G_GATE else ACT.Sigmoid
+                )
+                at = at + dest.shape[1]
+
+        make_gate(Q_GATE, 0, "a", [stretch(2)])
+        make_gate(G_GATE, 0, "b", [g_gate[:, 0:RUN]])
+        make_gate(F_GATE, 0, "c", [stretch(1)])
+        make_gate(F_GATE, RUN, "d", [stretch(4)])
+        make_gate(Q_GATE, RUN, "e", [stretch(3)])
+        make_gate(G_GATE, RUN, "f", [g_gate[:, RUN:HALF]])
+        make_gate(F_GATE, HALF, "a", [f_late[:, 0:RUN]])
+        make_gate(F_GATE, FUSED, "b", [f_late[:, RUN:HALF]])
         nc.scalar.activation(picked[:], cell_sb[:].indirect(entries(FUSED, S)), ACT.Copy)
+        make_gate(G_GATE, HALF, "g", [g_gate[:, HALF:S]])
 
         def fused(first, f_cols):
             nc.vector.tensor_tensor(
@@ -172,15 +179,17 @@ def tile_picked_beamcell_none_l_kernel(
         def store(first, end):
             nc.sync.dma_start(out=out[:, first:end], in_=result[:, first:end])
 
-        nc.vector.tensor_tensor(early[:, 0:RUN], early[:, 2 * RUN:3 * RUN], g_gate[:, 0:RUN], ALU.mult)
-        fused(0, early[:, RUN:2 * RUN])
-        fused(RUN, early[:, 4 * RUN:5 * RUN])
-        nc.vector.tensor_tensor(early[:, RUN:HALF], early[:, 3 * RUN:4 * RUN], g_gate[:, RUN:HALF], ALU.mult)
-        fused(HALF, late[:, F_GATE, 0:RUN])
+        nc.vector.tensor_tensor(stretch(0), stretch(2), g_gate[:, 0:RUN], ALU.mult)
+        fused(0, stretch(1))
+        fused(RUN, stretch(4))
+        nc.vector.tensor_tensor(stretch(1), stretch(3), g_gate[:, RUN:HALF], ALU.mult)
+        make_gate(Q_GATE, HALF, "h", [stretch(4), stretch(3)])
+        fused(HALF, f_late[:, 0:RUN])
         nc.vector.tensor_tensor(result[:, 0:HALF], kept[:, 0:HALF], early[:, 0:HALF], ALU.add)
         store(0, HALF)
-        nc.vector.tensor_tensor(result[:, HALF:S], late[:, Q_GATE, :], g_gate[:, HALF:S], ALU.mult)
-        nc.vector.tensor_tensor(kept[:, FUSED:S], picked[:], late[:, F_GATE, RUN:HALF], ALU.mult)
+        nc.vector.tensor_tensor(kept[:, FUSED:S], picked[:], f_late[:, RUN:HALF], ALU.mult)
+        nc.vector.tensor_tensor(result[:, HALF:FUSED], stretch(4), g_gate[:, HALF:FUSED], ALU.mult)
+        nc.vector.tensor_tensor(result[:, FUSED:S], stretch(3), g_gate[:, FUSED:S], ALU.mult)
         for first in (HALF, FUSED):
             cols = slice(first, first + RUN)
             nc.vector.tensor_tensor(result[:, cols], kept[:, cols], result[:, cols], ALU.add)

from contextlib import ExitStack

import concourse.mybir as mybir

K, T, S, N = 512, 2048, 1024, 128
FLOPS = 3 * 2 * K * N * S

F32 = mybir.dt.float32
BF16 = mybir.dt.bfloat16
I32 = mybir.dt.int32
U32 = mybir.dt.uint32
U16 = mybir.dt.uint16
U8 = mybir.dt.uint8
FP8X4 = mybir.dt.float8_e4m3fn_x4
ACT = mybir.ActivationFunctionType
ALU = mybir.AluOpType

P = 128
RUN = 256
F_GATE, Q_GATE, G_GATE = 0, 1, 2
HALF = 512
EARLY_OWN = 384
STEP = (640, 1024)
LAST_LOADS = (0, 1536, 2048)
ROUND_ON_SCALAR = 448
FUSED = 768


def tile_picked_beamcell_none_l_kernel(
    tc, xT, w1_words, w1_scales, w2_words, w2_scales, w3_words, w3_scales, cell, offs, out
):
    nc = tc.nc
    with ExitStack() as ctx:
        keep = ctx.enter_context(tc.tile_pool(name="keep", bufs=1))
        psum = ctx.enter_context(tc.psum_pool(name="psum", bufs=1))

        w_scales = keep.tile([P, 3 * N], U8, name="w_scales", align_bytes=64)
        nc.vector.memset(w_scales[:].bitcast(I32), 0)

        warm = keep.tile([P, 2], F32, name="warm")
        nc.vector.memset(warm[:, 0:1], 0.0)
        nc.scalar.activation(warm[:, 1:2], warm[:, 0:1], ACT.Sigmoid)

        raw = [keep.tile([P, T], F32, name="raw_%d" % t) for t in range(4)]
        rounded = keep.tile([P, T], BF16, name="rounded", align_bytes=64)
        offsets = keep.tile([P, S // 16], U16, name="offsets")
        w_codes = keep.tile([P, 3, N], U32, name="w_codes", align_bytes=64)
        cell_sb = keep.tile([P, T], F32, name="cell_sb")
        x_rows = xT.rearrange("(p t) c -> p t c", t=4)

        def load_codes(gate, words):
            nc.sync.dma_start(
                out=w_codes[:, gate, :].bitcast(I32), in_=words[0].rearrange("p n t -> p (n t)").bitcast(I32)
            )

        def move_scales(quadrant):
            nc.sync.dma_start(
                out=w_scales[32 * quadrant:32 * quadrant + 4, :].bitcast(I32),
                in_=w_scales[4 * quadrant:4 * quadrant + 4, :].bitcast(I32),
            )

        nc.sync.dma_start(out=raw[0][:], in_=x_rows[:, 0, :])
        nc.sync.dma_start(offsets[:], offs)
        for gate, scales in enumerate((w1_scales, w2_scales, w3_scales)):
            nc.sync.dma_start(out=w_scales[0:16, gate * N:(gate + 1) * N].bitcast(I32), in_=scales[0].bitcast(I32))
        nc.sync.dma_start(out=raw[1][:], in_=x_rows[:, 1, :])
        nc.sync.dma_start(out=raw[2][:], in_=x_rows[:, 2, :])
        move_scales(1)
        for first, end in zip(LAST_LOADS[:-1], LAST_LOADS[1:]):
            nc.sync.dma_start(out=raw[3][:, first:end], in_=x_rows[:, 3, first:end])
        load_codes(F_GATE, w1_words)
        load_codes(Q_GATE, w2_words)
        load_codes(G_GATE, w3_words)
        for quadrant in range(2, 4):
            move_scales(quadrant)
        nc.sync.dma_start(out=cell_sb[:], in_=cell)

        def entries(first, end):
            return offsets[:, first // 16:end // 16]

        woven = keep.tile([P, S, 4], BF16, name="woven", align_bytes=64)
        planes = [keep.tile([P, 2, S], BF16, name="planes_%d" % pair, align_bytes=64) for pair in range(2)]
        x_codes = keep.tile([P, S], U32, name="x_codes", align_bytes=64)
        x_scales = keep.tile([P, S], U8, name="x_scales", align_bytes=64)

        def gather_woven(t, first, end):
            nc.vector.tensor_copy(woven[:, first:end, t], raw[t][:].indirect(entries(first, end)))

        def gather_plane(t, first, end):
            nc.scalar.activation(planes[t // 2][:, t % 2, first:end], raw[t][:].indirect(entries(first, end)), ACT.Copy)

        def place(pair, first, end):
            nc.vector.tensor_copy(
                woven[:, first:end, 2 * pair:2 * pair + 2], planes[pair][:, :, first:end].rearrange("p t n -> p n t")
            )

        def quantise(first, end):
            cols = slice(first, end)
            nc.vector.quantize_mx(
                out=x_codes[:, cols].bitcast(FP8X4),
                scales=x_scales[:, cols],
                in_=woven[:, cols, :].rearrange("p n t -> p (n t)"),
            )

        def round_on_gpsimd(first, end):
            nc.gpsimd.tensor_scalar(rounded[:, first:end], raw[3][:, first:end], 1.0, 0.0, ALU.mult, ALU.add)

        gather_woven(0, 0, EARLY_OWN)
        gather_plane(0, EARLY_OWN, S)
        gather_woven(1, 0, EARLY_OWN)
        for first, end in ((EARLY_OWN, 704), (704, S)):
            gather_plane(1, first, end)
            place(0, first, end)

        gather_woven(2, 0, RUN)
        gather_plane(2, STEP[0], STEP[1])
        gather_plane(2, RUN, STEP[0])
        nc.vector.tensor_copy(woven[:, STEP[0]:STEP[1], 2], planes[1][:, 0, STEP[0]:STEP[1]])
        nc.scalar.copy(rounded[:, 0:ROUND_ON_SCALAR], raw[3][:, 0:ROUND_ON_SCALAR])
        nc.vector.tensor_copy(rounded[:, ROUND_ON_SCALAR:LAST_LOADS[1]], raw[3][:, ROUND_ON_SCALAR:LAST_LOADS[1]])
        round_on_gpsimd(LAST_LOADS[1], T)

        gather_woven(3, 0, RUN)
        for first, end in ((RUN, 320), (320, STEP[0])):
            gather_plane(3, first, end)
        nc.scalar.activation(woven[:, STEP[0]:STEP[1], 3], rounded[:].indirect(entries(STEP[0], STEP[1])), ACT.Copy)
        place(1, RUN, 320)
        quantise(0, RUN)
        place(1, 320, 2 * RUN)
        place(1, 2 * RUN, STEP[0])
        quantise(RUN, HALF)
        quantise(HALF, S)

        early = keep.tile([P, 5 * RUN], F32, name="early")
        f_late = keep.tile([P, HALF], F32, name="f_late")
        g_gate = keep.tile([P, S], F32, name="g_gate")
        picked = keep.tile([P, S - FUSED], F32, name="picked")
        kept = keep.tile([P, S], F32, name="kept")
        result = keep.tile([P, S], F32, name="result")

        def stretch(place):
            return early[:, place * RUN:(place + 1) * RUN]

        def make_gate(gate, first, bank_tag, dests):
            width = sum(dest.shape[1] for dest in dests)
            bank = psum.tile([P, width], F32, name="bank_%d_%d" % (gate, first), tag=bank_tag)
            nc.tensor.matmul_mx(
                out=bank[:],
                lhsT=w_codes[:, gate, :].bitcast(FP8X4),
                lhsT_scale=w_scales[:, gate * N:(gate + 1) * N],
                rhs=x_codes[:, first:first + width].bitcast(FP8X4),
                rhs_scale=x_scales[:, first:first + width],
                start=True,
                stop=True,
            )
            at = 0
            for dest in dests:
                nc.scalar.activation(
                    dest, bank[:, at:at + dest.shape[1]], ACT.Tanh if gate == G_GATE else ACT.Sigmoid
                )
                at = at + dest.shape[1]

        make_gate(Q_GATE, 0, "a", [stretch(2)])
        make_gate(G_GATE, 0, "b", [g_gate[:, 0:RUN]])
        make_gate(F_GATE, 0, "c", [stretch(1)])
        make_gate(F_GATE, RUN, "d", [stretch(4)])
        make_gate(Q_GATE, RUN, "e", [stretch(3)])
        make_gate(G_GATE, RUN, "f", [g_gate[:, RUN:HALF]])
        make_gate(F_GATE, HALF, "a", [f_late[:, 0:RUN]])
        make_gate(F_GATE, FUSED, "b", [f_late[:, RUN:HALF]])
        nc.scalar.activation(picked[:], cell_sb[:].indirect(entries(FUSED, S)), ACT.Copy)
        make_gate(G_GATE, HALF, "g", [g_gate[:, HALF:S]])

        def fused(first, f_cols):
            nc.vector.tensor_tensor(
                kept[:, first:first + RUN], cell_sb[:].indirect(entries(first, first + RUN)), f_cols, ALU.mult
            )

        def store(first, end):
            nc.sync.dma_start(out=out[:, first:end], in_=result[:, first:end])

        nc.vector.tensor_tensor(stretch(0), stretch(2), g_gate[:, 0:RUN], ALU.mult)
        fused(0, stretch(1))
        fused(RUN, stretch(4))
        nc.vector.tensor_tensor(stretch(1), stretch(3), g_gate[:, RUN:HALF], ALU.mult)
        make_gate(Q_GATE, HALF, "h", [stretch(4), stretch(3)])
        fused(HALF, f_late[:, 0:RUN])
        nc.vector.tensor_tensor(result[:, 0:HALF], kept[:, 0:HALF], early[:, 0:HALF], ALU.add)
        store(0, HALF)
        nc.vector.tensor_tensor(kept[:, FUSED:S], picked[:], f_late[:, RUN:HALF], ALU.mult)
        nc.vector.tensor_tensor(result[:, HALF:FUSED], stretch(4), g_gate[:, HALF:FUSED], ALU.mult)
        nc.vector.tensor_tensor(result[:, FUSED:S], stretch(3), g_gate[:, FUSED:S], ALU.mult)
        for first in (HALF, FUSED):
            cols = slice(first, first + RUN)
            nc.vector.tensor_tensor(result[:, cols], kept[:, cols], result[:, cols], ALU.add)
            store(first, first + RUN)
